import numpy as np
import ml_dtypes


def mxq(x, axis, fmt="e4m3"):
    dtype, down = {"e4m3": (ml_dtypes.float8_e4m3fn, 7), "e5m2": (ml_dtypes.float8_e5m2, 14)}[fmt]
    v = np.moveaxis(np.asarray(x, np.float32).astype(ml_dtypes.bfloat16).astype(np.float64), axis, -1)
    blocks = v.reshape(v.shape[:-1] + (-1, 32))
    amax = np.abs(blocks).max(-1, keepdims=True)
    byte = np.maximum(np.where(amax > 0, np.frexp(amax)[1] - 1 + 127, 0) - down, 1)
    scale = np.exp2(byte - 127.0)
    codes = (blocks / scale).astype(np.float32).astype(dtype).astype(np.float64)
    return np.moveaxis((codes * scale).reshape(v.shape), -1, axis)


WIDE = False


def mx_kscale(k):
    if not WIDE:
        return np.ones(k)
    levels = np.array([10, -10, 5, -5, 0])
    if k % 512:
        return np.exp2(np.random.permutation(np.resize(levels, k // 32))).repeat(32)
    a = np.empty((k // 512, 16))
    for p in range(k // 512):
        a[p, :8] = np.random.permutation(np.resize(levels, 8))
        for g in range(8):
            far = levels[np.abs(levels - a[p, g]) >= 10]
            a[p, g + 8] = far[np.random.randint(len(far))]
    return np.exp2(a.ravel()).repeat(32)


def f64(x):
    return np.asarray(x).astype(np.float64)


def striped(idx):
    return np.tile(idx.reshape(-1, 16).T, (8, 1)).astype(np.uint16)


def unstriped(offs):
    return offs[:16].T.reshape(-1).astype(np.int64)


E2M1 = np.array([0.0, 0.5, 1.0, 1.5, 2.0, 3.0, 4.0, 6.0, -0.0, -0.5, -1.0, -1.5, -2.0, -3.0, -4.0, -6.0])


def pack_weight(w, fmt):
    k, n = w.shape
    w = f64(np.asarray(w, np.float32).astype(ml_dtypes.bfloat16)).reshape(k // 32, 32, n)
    amax = np.abs(w).max(1)
    if fmt == "e4m3":
        byte = np.frexp(amax)[1] - 1 + 127 - 7
    else:
        mant, ex = np.frexp(amax / 6.0)
        byte = np.where(mant > 0.5, ex, ex - 1) + 127
    byte = np.clip(np.where(amax > 0, byte, 1), 1, 254)
    scaled = (w * np.exp2(127.0 - byte)[:, None, :]).reshape(k, n).astype(np.float32)
    by_word = np.ascontiguousarray(scaled.reshape(k // 512, 128, 4, n).transpose(0, 1, 3, 2))
    if fmt == "e4m3":
        words = by_word.astype(ml_dtypes.float8_e4m3fn).view(np.uint8)
    else:
        c = by_word.astype(ml_dtypes.float4_e2m1fn).view(np.uint8) & 0xF
        words = (c[..., 0::2] | (c[..., 1::2] << 4)).reshape(k // 512, 128, 2 * n)
    return np.ascontiguousarray(words), np.ascontiguousarray(byte.astype(np.uint8).reshape(k // 512, 16, n))


def unpack_weight(words, scales, fmt):
    g, _, n = scales.shape
    words = np.ascontiguousarray(words).reshape(g, 128, n, -1)
    if fmt == "e4m3":
        vals = words.view(ml_dtypes.float8_e4m3fn).astype(np.float64)
    else:
        nib = np.empty((g, 128, n, 4), np.uint8)
        nib[..., 0::2] = words & 0xF
        nib[..., 1::2] = words >> 4
        vals = E2M1[nib]
    vals = vals * np.repeat(np.exp2(scales.astype(np.float64) - 127.0), 8, axis=1)[..., None]
    return vals.transpose(0, 1, 3, 2).reshape(g * 512, n)


def gelu(v):
    return 0.5 * v * (1.0 + np.tanh(np.sqrt(2.0 / np.pi) * (v + 0.044715 * v**3)))


T, S, P, K, H = 2048, 1024, 512, 1536, 1024

def setup_inputs():
    n = np.random.standard_normal
    s = mx_kscale(K)[:, None]
    u = mx_kscale(H)[:, None]
    tab_words, tab_scales = pack_weight(n((K, T)) * s, "e4m3")
    w2_words, w2_scales = pack_weight(n((H, H)) / np.sqrt(H) / u, "e2m1")
    return {
        "tab_words": tab_words,
        "tab_scales": tab_scales,
        "offs": striped(np.random.permutation(T)[:S]),
        "pos1": striped(np.random.permutation(S)[:P]),
        "pos2": striped(np.random.permutation(S)[:P]),
        "w1": (n((K, H)) / np.sqrt(K) / s).astype(np.float32),
        "gain": (np.exp(0.3 * n(H)) * u[:, 0]).astype(np.float32),
        "w2_words": w2_words,
        "w2_scales": w2_scales,
    }

def reference(tab_words, tab_scales, offs, pos1, pos2, w1, gain, w2_words, w2_scales):
    v = unpack_weight(tab_words, tab_scales, "e4m3")[:, unstriped(offs)]
    w1q = mxq(f64(w1), 0, "e4m3")
    h = w1q.T @ v
    x = h[:, unstriped(pos1)]
    z = f64(gain)[:, None] / (1.0 + np.square(x))
    zq = mxq(z, 0, "e4m3")
    w2 = unpack_weight(w2_words, w2_scales, "e2m1")
    y = w2.T @ zq
    return y * h[:, unstriped(pos2)]

@@ -1,0 +1,246 @@
+from contextlib import ExitStack
+
+import concourse.mybir as mybir
+from concourse.masks import make_identity
+
+T, S, PAIRS, K, H = 2048, 1024, 512, 1536, 1024
+FLOPS = 2 * K * H * S + 2 * H * H * PAIRS
+
+F32 = mybir.dt.float32
+BF16 = mybir.dt.bfloat16
+I32 = mybir.dt.int32
+U32 = mybir.dt.uint32
+U16 = mybir.dt.uint16
+U8 = mybir.dt.uint8
+FP8X4 = mybir.dt.float8_e4m3fn_x4
+FP4X4 = mybir.dt.float4_e2m1fn_x4
+ACT = mybir.ActivationFunctionType
+MULT = mybir.AluOpType.mult
+
+P = 128
+PACK = 4
+K_PASS = P * PACK
+BANK = 512
+PASSES1 = K // K_PASS
+PASSES2 = H // K_PASS
+TILES = H // P
+GROUP = 2
+GROUPS = TILES // GROUP
+GCOLS = GROUP * P
+HALVES = S // BANK
+EARLY = 6
+
+
+def tile_list_dye_inhibition_kernel(
+    tc, tab_words, tab_scales, offs, pos1, pos2, w1, gain, w2_words, w2_scales, out
+):
+    nc = tc.nc
+    with ExitStack() as ctx:
+        keep = ctx.enter_context(tc.tile_pool(name="keep", bufs=1))
+        psum = ctx.enter_context(tc.psum_pool(name="psum", bufs=1))
+
+        def kept(shape, dtype, name, tag=None):
+            return keep.tile(shape, dtype, name=name, tag=tag or name, align_bytes=64)
+
+        def bank(index, name):
+            return psum.tile([P, BANK], F32, name=name, tag="bank%d" % index)
+
+        offs_sb = kept([P, S // 16], U16, "offs_sb")
+        pos1_sb = kept([P, PAIRS // 16], U16, "pos1_sb")
+        pos2_sb = kept([P, PAIRS // 16], U16, "pos2_sb")
+        tab_plane = kept([P, T], U8, "tab_plane")
+        w2_plane = kept([P, PASSES2, H], U8, "w2_plane")
+        gain_rows = kept([P, P], F32, "gain_rows")
+        ident = kept([P, P], F32, "ident")
+        warm = kept([P, 2], F32, "warm")
+
+        nc.gpsimd.memset(tab_plane[:].bitcast(I32), 0)
+        nc.vector.memset(warm[:], 1.0)
+        nc.vector.memset(w2_plane[:].rearrange("p a c -> p (a c)").bitcast(I32), 0)
+        nc.gpsimd.memset(gain_rows[:], 0.0)
+        make_identity(nc, ident[:])
+
+        nc.scalar.activation(warm[:, 1:2], warm[:, 0:1], ACT.Abs_reciprocal_sqrt)
+
+        tab = {}
+        raw = {}
+
+        def load_w1(a, g):
+            raw[a, g] = kept([P, PACK, GCOLS], F32, "raw_%d_%d" % (a, g))
+            rows = w1[a * K_PASS : (a + 1) * K_PASS, g * GCOLS : (g + 1) * GCOLS]
+            nc.sync.dma_start(out=raw[a, g][:], in_=rows.rearrange("(p j) c -> p j c", j=PACK))
+
+        def load_table(a):
+            tab[a] = kept([P, T], I32, "tab_%d" % a)
+            nc.sync.dma_start(out=tab[a][:], in_=tab_words[a].rearrange("p t i -> p (t i)").bitcast(I32))
+
+        load_table(0)
+        nc.sync.dma_start(offs_sb[:], offs)
+        load_table(1)
+        for q in range(4):
+            nc.sync.dma_start(
+                out=tab_plane[:].bitcast(I32)[32 * q : 32 * q + 4 * PASSES1, :],
+                in_=tab_scales.bitcast(I32)[:, 4 * q : 4 * q + 4, :],
+            )
+        load_w1(0, 0)
+        nc.sync.dma_start(out=gain_rows[0:TILES, :], in_=gain.rearrange("(i q) -> i q", q=P))
+        load_w1(1, 0)
+        load_w1(2, 0)
+        load_table(2)
+        nc.sync.dma_start(pos1_sb[:], pos1)
+        for g in range(1, GROUPS):
+            for a in range(PASSES1):
+                load_w1(a, g)
+        nc.sync.dma_start(pos2_sb[:], pos2)
+        w2_sb = kept([P, PASSES2, 2 * H // 4], I32, "w2_sb")
+        nc.sync.dma_start(out=w2_sb[:], in_=w2_words.bitcast(I32).rearrange("a p c -> p a c"))
+        for q in range(4):
+            nc.sync.dma_start(
+                out=w2_plane[:].bitcast(I32)[32 * q : 32 * q + 4, :, :],
+                in_=w2_scales.bitcast(I32)[:, 4 * q : 4 * q + 4, :].rearrange("a r c -> r a c"),
+            )
+
+        gain_ps = bank(7, "gain_ps")
+        nc.tensor.transpose(gain_ps[:, 0:P], gain_rows[:], ident[:])
+        gain_sb = kept([P, TILES], F32, "gain_sb")
+        nc.scalar.copy(gain_sb[:], gain_ps[:, 0:TILES])
+
+        v_plane = {}
+        v_words = {}
+
+        def offs_half(hh):
+            return offs_sb[:, hh * (BANK // 16) : (hh + 1) * (BANK // 16)]
+
+        def gather_words(a, hh):
+            v_words[a, hh] = kept([P, BANK], U32, "v_words_%d_%d" % (a, hh))
+            nc.vector.tensor_copy(v_words[a, hh][:], tab[a][:].bitcast(U32).indirect(offs_half(hh)))
+
+        for hh in range(HALVES):
+            v_plane[hh] = kept([P, BANK], U8, "v_plane_%d" % hh)
+            nc.vector.tensor_copy(v_plane[hh][:], tab_plane[:].indirect(offs_half(hh)))
+
+        w_codes = {}
+        w_plane = {}
+        acc = {}
+
+        def quantise_w1(a, g):
+            grouped = kept([P, GCOLS, PACK], BF16, "grouped_%d_%d" % (a, g))
+            dst = grouped[:].rearrange("p (c i) j -> p c j i", i=4)
+            src = raw[a, g][:].rearrange("p j (c i) -> p c j i", i=4)
+            if a > 0 and g > 0:
+                nc.vector.tensor_copy(dst, src)
+            else:
+                nc.scalar.copy(dst, src)
+            w_codes[a, g] = kept([P, GCOLS], U32, "w_codes_%d_%d" % (a, g))
+            w_plane[a, g] = kept([P, GCOLS], U8, "w_plane_%d_%d" % (a, g))
+            nc.vector.quantize_mx(
+                out=w_codes[a, g][:].bitcast(FP8X4),
+                scales=w_plane[a, g][:],
+                in_=grouped[:].rearrange("p c j -> p (c j)"),
+            )
+
+        def stage1_pass(a, g, hh):
+            for u in range(GROUP):
+                i = g * GROUP + u
+                if a == 0:
+                    acc[i, hh] = bank((g % 2) * 4 + 2 * u + hh, "acc_%d_%d" % (i, hh))
+                cols = slice(u * P, (u + 1) * P)
+                nc.tensor.matmul_mx(
+                    out=acc[i, hh][:],
+                    lhsT=w_codes[a, g][:, cols].bitcast(FP8X4),
+                    lhsT_scale=w_plane[a, g][:, cols],
+                    rhs=v_words[a, hh][:].bitcast(FP8X4),
+                    rhs_scale=v_plane[hh][4 * a :, :],
+                    start=(a == 0),
+                    stop=(a == PASSES1 - 1),
+                )
+
+        h = {}
+        z_rows = {b: kept([P, PACK, PAIRS], BF16, "z_rows_%d" % b) for b in range(PASSES2)}
+
+        def scores(g):
+            for u in range(GROUP):
+                i = g * GROUP + u
+                h[i] = kept([P, S], F32, "h_%d" % i)
+            for u in range(GROUP):
+                i = g * GROUP + u
+                for hh in range(HALVES):
+                    nc.scalar.copy(h[i][:, hh * BANK : (hh + 1) * BANK], acc[i, hh][:])
+
+        def damping(i):
+            x = kept([P, PAIRS], F32, "x_%d" % i)
+            nc.vector.tensor_copy(x[:], h[i][:].indirect(pos1_sb[:]))
+            sq = kept([P, PAIRS], F32, "sq_%d" % i, tag="sq")
+            nc.scalar.activation(sq[:], x[:], ACT.Square)
+            root = kept([P, PAIRS], F32, "root_%d" % i, tag="root_%d" % (i % 2))
+            nc.scalar.activation(root[:], sq[:], ACT.Abs_reciprocal_sqrt, bias=1.0)
+            z = kept([P, PAIRS], BF16, "z_%d" % i)
+            nc.vector.scalar_tensor_tensor(z[:], root[:], gain_sb[:, i : i + 1], root[:], MULT, MULT)
+            b, part = divmod(i, PACK)
+            nc.sync.dma_start(out=z_rows[b][32 * part : 32 * part + 32, :, :], in_=z[:])
+
+        for a in range(PASSES1):
+            quantise_w1(a, 0)
+            for hh in range(HALVES):
+                gather_words(a, hh)
+                stage1_pass(a, 0, hh)
+        for g in range(GROUPS):
+            scores(g)
+            if g + 1 < GROUPS:
+                for a in range(PASSES1):
+                    quantise_w1(a, g + 1)
+                    for hh in range(HALVES):
+                        stage1_pass(a, g + 1, hh)
+            for u in range(GROUP):
+                damping(g * GROUP + u)
+
+        y = {}
+        h2 = {}
+
+        def pick_targets(tiles, tag):
+            picked = kept([P, len(tiles), PAIRS], F32, "h2_%d" % tiles[0], tag=tag)
+            for u, i in enumerate(tiles):
+                h2[i] = picked[:, u, :]
+                nc.vector.tensor_copy(h2[i], h[i][:].indirect(pos2_sb[:]))
+
+        pick_targets((0,), "x_4")
+        pick_targets((1,), "x_6")
+        pick_targets((2, 3), "root_1")
+        for b in range(PASSES2):
+            tag = "sq" if b == 0 else None
+            z_grouped = kept([P, PAIRS, PACK], BF16, "z_grouped_%d" % b, tag=tag)
+            nc.scalar.copy(
+                z_grouped[:].rearrange("p (c i) j -> p c j i", i=4),
+                z_rows[b][:].rearrange("p j (c i) -> p c j i", i=4),
+            )
+            z_codes = kept([P, PAIRS], U32, "z_codes_%d" % b)
+            z_plane = kept([P, PAIRS], U8, "z_plane_%d" % b)
+            nc.vector.quantize_mx(
+                out=z_codes[:].bitcast(FP8X4),
+                scales=z_plane[:],
+                in_=z_grouped[:].rearrange("p c j -> p (c j)"),
+            )
+            for i in range(TILES):
+                if b == 0:
+                    y[i] = bank(i, "y_%d" % i)
+                nc.tensor.matmul_mx(
+                    out=y[i][:],
+                    lhsT=w2_sb[:, b, :].bitcast(U8)[:, 2 * i * P : 2 * (i + 1) * P].bitcast(FP4X4),
+                    lhsT_scale=w2_plane[:, b, i * P : (i + 1) * P],
+                    rhs=z_codes[:].bitcast(FP8X4),
+                    rhs_scale=z_plane[:],
+                    start=(b == 0),
+                    stop=(b == PASSES2 - 1),
+                )
+            if b == 0:
+                pick_targets((4, 5), "sq")
+
+        for i in range(TILES):
+            res = kept([P, PAIRS], F32, "res_%d" % i, tag="raw_%d_%d" % (i % PASSES1, i // PASSES1))
+            if i < EARLY:
+                nc.vector.tensor_tensor(res[:], y[i][:], h2[i], MULT)
+            else:
+                y_sb = kept([P, PAIRS], F32, "y_sb_%d" % i)
+                nc.scalar.copy(y_sb[:], y[i][:])
+                nc.vector.tensor_tensor(res[:], h[i][:].indirect(pos2_sb[:]), y_sb[:], MULT)
+            nc.sync.dma_start(out=out[i * P : (i + 1) * P, :], in_=res[:])

@@ -28,7 +28,10 @@ GROUP = 2
 GROUPS = TILES // GROUP
 GCOLS = GROUP * P
 HALVES = S // BANK
-EARLY = 6
+EARLY = 5
+HALF = PAIRS // 2
+SCALAR_CASTS = 5
+Y_ORDER = (0, 1) + tuple(range(EARLY, TILES)) + tuple(range(2, EARLY))
 
 
 def tile_list_dye_inhibition_kernel(
@@ -112,7 +115,7 @@ def tile_list_dye_inhibition_kernel(
             return offs_sb[:, hh * (BANK // 16) : (hh + 1) * (BANK // 16)]
 
         def gather_words(a, hh):
-            v_words[a, hh] = kept([P, BANK], U32, "v_words_%d_%d" % (a, hh))
+            v_words[a, hh] = kept([P, BANK], U32, "v_words_%d_%d" % (a, hh), tag="grouped_1_0" if (a, hh) == (1, 1) else None)
             nc.vector.tensor_copy(v_words[a, hh][:], tab[a][:].bitcast(U32).indirect(offs_half(hh)))
 
         for hh in range(HALVES):
@@ -123,20 +126,26 @@ def tile_list_dye_inhibition_kernel(
         w_plane = {}
         acc = {}
 
-        def quantise_w1(a, g):
-            grouped = kept([P, GCOLS, PACK], BF16, "grouped_%d_%d" % (a, g))
-            dst = grouped[:].rearrange("p (c i) j -> p c j i", i=4)
+        grouped = {}
+
+        def round_w1(a, g):
+            grouped[a, g] = kept([P, GCOLS, PACK], BF16, "grouped_%d_%d" % (a, g))
+            dst = grouped[a, g][:].rearrange("p (c i) j -> p c j i", i=4)
             src = raw[a, g][:].rearrange("p j (c i) -> p c j i", i=4)
-            if a > 0 and g > 0:
+            if a > 0 and g * PASSES1 + a >= SCALAR_CASTS:
                 nc.vector.tensor_copy(dst, src)
             else:
                 nc.scalar.copy(dst, src)
+
+        def quantise_w1(a, g):
+            if (a, g) not in grouped:
+                round_w1(a, g)
             w_codes[a, g] = kept([P, GCOLS], U32, "w_codes_%d_%d" % (a, g))
             w_plane[a, g] = kept([P, GCOLS], U8, "w_plane_%d_%d" % (a, g))
             nc.vector.quantize_mx(
                 out=w_codes[a, g][:].bitcast(FP8X4),
                 scales=w_plane[a, g][:],
-                in_=grouped[:].rearrange("p c j -> p (c j)"),
+                in_=grouped[a, g][:].rearrange("p c j -> p (c j)"),
             )
 
         def stage1_pass(a, g, hh):
@@ -168,11 +177,15 @@ def tile_list_dye_inhibition_kernel(
                     nc.scalar.copy(h[i][:, hh * BANK : (hh + 1) * BANK], acc[i, hh][:])
 
         def damping(i):
-            x = kept([P, PAIRS], F32, "x_%d" % i)
+            g, u = divmod(i, GROUP)
+            tag = None
+            if i > 0 and g + 1 < GROUPS:
+                tag = ("w_codes_%d_%d", "w_plane_%d_%d")[u] % (PASSES1 - 1, g + 1)
+            x = kept([P, PAIRS], F32, "x_%d" % i, tag=tag)
             nc.vector.tensor_copy(x[:], h[i][:].indirect(pos1_sb[:]))
-            sq = kept([P, PAIRS], F32, "sq_%d" % i, tag="sq")
+            sq = kept([P, PAIRS], F32, "sq_%d" % i, tag="sq_%d" % u)
             nc.scalar.activation(sq[:], x[:], ACT.Square)
-            root = kept([P, PAIRS], F32, "root_%d" % i, tag="root_%d" % (i % 2))
+            root = kept([P, PAIRS], F32, "root_%d" % i)
             nc.scalar.activation(root[:], sq[:], ACT.Abs_reciprocal_sqrt, bias=1.0)
             z = kept([P, PAIRS], BF16, "z_%d" % i)
             nc.vector.scalar_tensor_tensor(z[:], root[:], gain_sb[:, i : i + 1], root[:], MULT, MULT)
@@ -184,13 +197,22 @@ def tile_list_dye_inhibition_kernel(
             for hh in range(HALVES):
                 gather_words(a, hh)
                 stage1_pass(a, 0, hh)
+
+        def prepare(g):
+            for a in range(PASSES1):
+                quantise_w1(a, g)
+                for hh in range(HALVES):
+                    stage1_pass(a, g, hh)
+
+        prepare(1)
+        scores(0)
         for g in range(GROUPS):
-            scores(g)
+            if g + 2 < GROUPS:
+                prepare(g + 2)
+            if g + 3 < GROUPS:
+                round_w1(0, g + 3)
             if g + 1 < GROUPS:
-                for a in range(PASSES1):
-                    quantise_w1(a, g + 1)
-                    for hh in range(HALVES):
-                        stage1_pass(a, g + 1, hh)
+                scores(g + 1)
             for u in range(GROUP):
                 damping(g * GROUP + u)
 
@@ -203,11 +225,9 @@ def tile_list_dye_inhibition_kernel(
                 h2[i] = picked[:, u, :]
                 nc.vector.tensor_copy(h2[i], h[i][:].indirect(pos2_sb[:]))
 
-        pick_targets((0,), "x_4")
-        pick_targets((1,), "x_6")
-        pick_targets((2, 3), "root_1")
+        pick_targets((0, 1), "root_7")
         for b in range(PASSES2):
-            tag = "sq" if b == 0 else None
+            tag = "sq_1" if b == 0 else "z_grouped_1"
             z_grouped = kept([P, PAIRS, PACK], BF16, "z_grouped_%d" % b, tag=tag)
             nc.scalar.copy(
                 z_grouped[:].rearrange("p (c i) j -> p c j i", i=4),
@@ -220,7 +240,7 @@ def tile_list_dye_inhibition_kernel(
                 scales=z_plane[:],
                 in_=z_grouped[:].rearrange("p c j -> p (c j)"),
             )
-            for i in range(TILES):
+            for i in Y_ORDER:
                 if b == 0:
                     y[i] = bank(i, "y_%d" % i)
                 nc.tensor.matmul_mx(
@@ -232,15 +252,18 @@ def tile_list_dye_inhibition_kernel(
                     start=(b == 0),
                     stop=(b == PASSES2 - 1),
                 )
-            if b == 0:
-                pick_targets((4, 5), "sq")
+            pick_targets((2, 3) if b == 0 else (4,), tag)
 
         for i in range(TILES):
             res = kept([P, PAIRS], F32, "res_%d" % i, tag="raw_%d_%d" % (i % PASSES1, i // PASSES1))
             if i < EARLY:
                 nc.vector.tensor_tensor(res[:], y[i][:], h2[i], MULT)
+                nc.sync.dma_start(out=out[i * P : (i + 1) * P, :], in_=res[:])
             else:
                 y_sb = kept([P, PAIRS], F32, "y_sb_%d" % i)
                 nc.scalar.copy(y_sb[:], y[i][:])
-                nc.vector.tensor_tensor(res[:], h[i][:].indirect(pos2_sb[:]), y_sb[:], MULT)
-            nc.sync.dma_start(out=out[i * P : (i + 1) * P, :], in_=res[:])
+                for s in range(2):
+                    cols = slice(s * HALF, (s + 1) * HALF)
+                    targets = h[i][:].indirect(pos2_sb[:, s * HALF // 16 : (s + 1) * HALF // 16])
+                    nc.vector.tensor_tensor(res[:, cols], targets, y_sb[:, cols], MULT)
+                    nc.sync.dma_start(out=out[i * P : (i + 1) * P, cols], in_=res[:, cols])

@@ -24,11 +24,11 @@ BANK = 512
 PASSES1 = K // K_PASS
 PASSES2 = H // K_PASS
 TILES = H // P
-GROUP = 2
-GROUPS = TILES // GROUP
-GCOLS = GROUP * P
+GROUPS = ((0, 1), (1, 3), (3, 5), (5, 7), (7, 8))
+LAST = len(GROUPS) - 1
 HALVES = S // BANK
-EARLY = 5
+EARLY = 6
+FREE = 0
 HALF = PAIRS // 2
 SCALAR_CASTS = 5
 Y_ORDER = (0, 1) + tuple(range(EARLY, TILES)) + tuple(range(2, EARLY))
@@ -69,8 +69,9 @@ def tile_list_dye_inhibition_kernel(
         raw = {}
 
         def load_w1(a, g):
-            raw[a, g] = kept([P, PACK, GCOLS], F32, "raw_%d_%d" % (a, g))
-            rows = w1[a * K_PASS : (a + 1) * K_PASS, g * GCOLS : (g + 1) * GCOLS]
+            first, end = GROUPS[g]
+            raw[a, g] = kept([P, PACK, (end - first) * P], F32, "raw_%d_%d" % (a, g))
+            rows = w1[a * K_PASS : (a + 1) * K_PASS, first * P : end * P]
             nc.sync.dma_start(out=raw[a, g][:], in_=rows.rearrange("(p j) c -> p j c", j=PACK))
 
         def load_table(a):
@@ -91,7 +92,7 @@ def tile_list_dye_inhibition_kernel(
         load_w1(2, 0)
         load_table(2)
         nc.sync.dma_start(pos1_sb[:], pos1)
-        for g in range(1, GROUPS):
+        for g in range(1, len(GROUPS)):
             for a in range(PASSES1):
                 load_w1(a, g)
         nc.sync.dma_start(pos2_sb[:], pos2)
@@ -108,19 +109,23 @@ def tile_list_dye_inhibition_kernel(
         gain_sb = kept([P, TILES], F32, "gain_sb")
         nc.scalar.copy(gain_sb[:], gain_ps[:, 0:TILES])
 
-        v_plane = {}
         v_words = {}
 
         def offs_half(hh):
             return offs_sb[:, hh * (BANK // 16) : (hh + 1) * (BANK // 16)]
 
-        def gather_words(a, hh):
-            v_words[a, hh] = kept([P, BANK], U32, "v_words_%d_%d" % (a, hh), tag="grouped_1_0" if (a, hh) == (1, 1) else None)
-            nc.vector.tensor_copy(v_words[a, hh][:], tab[a][:].bitcast(U32).indirect(offs_half(hh)))
+        def gather_words(a):
+            words = kept([P, S], U32, "v_words_%d" % a)
+            window = tab[a][:].bitcast(U32)
+            if a < PASSES1 - 1:
+                nc.vector.tensor_copy(words[:], window.indirect(offs_sb[:]))
+            for hh in range(HALVES):
+                v_words[a, hh] = words[:, hh * BANK : (hh + 1) * BANK]
+                if a == PASSES1 - 1:
+                    nc.vector.tensor_copy(v_words[a, hh], window.indirect(offs_half(hh)))
 
-        for hh in range(HALVES):
-            v_plane[hh] = kept([P, BANK], U8, "v_plane_%d" % hh)
-            nc.vector.tensor_copy(v_plane[hh][:], tab_plane[:].indirect(offs_half(hh)))
+        planes = kept([P, S], U8, "v_planes")
+        nc.vector.tensor_copy(planes[:], tab_plane[:].indirect(offs_sb[:]))
 
         w_codes = {}
         w_plane = {}
@@ -128,8 +133,11 @@ def tile_list_dye_inhibition_kernel(
 
         grouped = {}
 
+        def width(g):
+            return (GROUPS[g][1] - GROUPS[g][0]) * P
+
         def round_w1(a, g):
-            grouped[a, g] = kept([P, GCOLS, PACK], BF16, "grouped_%d_%d" % (a, g))
+            grouped[a, g] = kept([P, width(g), PACK], BF16, "grouped_%d_%d" % (a, g))
             dst = grouped[a, g][:].rearrange("p (c i) j -> p c j i", i=4)
             src = raw[a, g][:].rearrange("p j (c i) -> p c j i", i=4)
             if a > 0 and g * PASSES1 + a >= SCALAR_CASTS:
@@ -140,8 +148,8 @@ def tile_list_dye_inhibition_kernel(
         def quantise_w1(a, g):
             if (a, g) not in grouped:
                 round_w1(a, g)
-            w_codes[a, g] = kept([P, GCOLS], U32, "w_codes_%d_%d" % (a, g))
-            w_plane[a, g] = kept([P, GCOLS], U8, "w_plane_%d_%d" % (a, g))
+            w_codes[a, g] = kept([P, width(g)], U32, "w_codes_%d_%d" % (a, g))
+            w_plane[a, g] = kept([P, width(g)], U8, "w_plane_%d_%d" % (a, g))
             nc.vector.quantize_mx(
                 out=w_codes[a, g][:].bitcast(FP8X4),
                 scales=w_plane[a, g][:],
@@ -149,17 +157,16 @@ def tile_list_dye_inhibition_kernel(
             )
 
         def stage1_pass(a, g, hh):
-            for u in range(GROUP):
-                i = g * GROUP + u
+            for u, i in enumerate(range(*GROUPS[g])):
                 if a == 0:
-                    acc[i, hh] = bank((g % 2) * 4 + 2 * u + hh, "acc_%d_%d" % (i, hh))
+                    acc[i, hh] = bank((HALVES * i + hh) % 8, "acc_%d_%d" % (i, hh))
                 cols = slice(u * P, (u + 1) * P)
                 nc.tensor.matmul_mx(
                     out=acc[i, hh][:],
                     lhsT=w_codes[a, g][:, cols].bitcast(FP8X4),
                     lhsT_scale=w_plane[a, g][:, cols],
-                    rhs=v_words[a, hh][:].bitcast(FP8X4),
-                    rhs_scale=v_plane[hh][4 * a :, :],
+                    rhs=v_words[a, hh].bitcast(FP8X4),
+                    rhs_scale=planes[4 * a :, hh * BANK : (hh + 1) * BANK],
                     start=(a == 0),
                     stop=(a == PASSES1 - 1),
                 )
@@ -168,22 +175,19 @@ def tile_list_dye_inhibition_kernel(
         z_rows = {b: kept([P, PACK, PAIRS], BF16, "z_rows_%d" % b) for b in range(PASSES2)}
 
         def scores(g):
-            for u in range(GROUP):
-                i = g * GROUP + u
-                h[i] = kept([P, S], F32, "h_%d" % i)
-            for u in range(GROUP):
-                i = g * GROUP + u
+            for i in range(*GROUPS[g]):
+                h[i] = kept([P, S], F32, "h_%d" % i, tag="raw_0_1" if i == 0 else None)
                 for hh in range(HALVES):
                     nc.scalar.copy(h[i][:, hh * BANK : (hh + 1) * BANK], acc[i, hh][:])
 
-        def damping(i):
-            g, u = divmod(i, GROUP)
+        def damping(g, i):
+            u = i % 2
             tag = None
-            if i > 0 and g + 1 < GROUPS:
+            if i >= FREE and g < LAST:
                 tag = ("w_codes_%d_%d", "w_plane_%d_%d")[u] % (PASSES1 - 1, g + 1)
-            x = kept([P, PAIRS], F32, "x_%d" % i, tag=tag)
+            x = kept([P, PAIRS], F32, "x_%d" % i, tag="grouped_2_1" if i == 0 else None)
             nc.vector.tensor_copy(x[:], h[i][:].indirect(pos1_sb[:]))
-            sq = kept([P, PAIRS], F32, "sq_%d" % i, tag="sq_%d" % u)
+            sq = kept([P, PAIRS], F32, "sq_%d" % i, tag=tag or "sq_%d" % u)
             nc.scalar.activation(sq[:], x[:], ACT.Square)
             root = kept([P, PAIRS], F32, "root_%d" % i)
             nc.scalar.activation(root[:], sq[:], ACT.Abs_reciprocal_sqrt, bias=1.0)
@@ -193,10 +197,7 @@ def tile_list_dye_inhibition_kernel(
             nc.sync.dma_start(out=z_rows[b][32 * part : 32 * part + 32, :, :], in_=z[:])
 
         for a in range(PASSES1):
-            quantise_w1(a, 0)
-            for hh in range(HALVES):
-                gather_words(a, hh)
-                stage1_pass(a, 0, hh)
+            gather_words(a)
 
         def prepare(g):
             for a in range(PASSES1):
@@ -204,17 +205,20 @@ def tile_list_dye_inhibition_kernel(
                 for hh in range(HALVES):
                     stage1_pass(a, g, hh)
 
+        prepare(0)
         prepare(1)
         scores(0)
-        for g in range(GROUPS):
-            if g + 2 < GROUPS:
+        for g in range(len(GROUPS)):
+            if g + 2 <= LAST:
                 prepare(g + 2)
-            if g + 3 < GROUPS:
+            if g + 3 <= LAST:
                 round_w1(0, g + 3)
-            if g + 1 < GROUPS:
+            if g + 1 < LAST:
                 scores(g + 1)
-            for u in range(GROUP):
-                damping(g * GROUP + u)
+            if g + 2 == LAST:
+                scores(LAST)
+            for i in range(*GROUPS[g]):
+                damping(g, i)
 
         y = {}
         h2 = {}
@@ -225,6 +229,7 @@ def tile_list_dye_inhibition_kernel(
                 h2[i] = picked[:, u, :]
                 nc.vector.tensor_copy(h2[i], h[i][:].indirect(pos2_sb[:]))
 
+        pick_targets((5,), "root_4")
         pick_targets((0, 1), "root_7")
         for b in range(PASSES2):
             tag = "sq_1" if b == 0 else "z_grouped_1"
@@ -255,12 +260,12 @@ def tile_list_dye_inhibition_kernel(
             pick_targets((2, 3) if b == 0 else (4,), tag)
 
         for i in range(TILES):
-            res = kept([P, PAIRS], F32, "res_%d" % i, tag="raw_%d_%d" % (i % PASSES1, i // PASSES1))
+            res = kept([P, PAIRS], F32, "res_%d" % i, tag="raw_%d_%d" % (i % PASSES1, 2 + i // PASSES1))
             if i < EARLY:
                 nc.vector.tensor_tensor(res[:], y[i][:], h2[i], MULT)
                 nc.sync.dma_start(out=out[i * P : (i + 1) * P, :], in_=res[:])
             else:
-                y_sb = kept([P, PAIRS], F32, "y_sb_%d" % i)
+                y_sb = kept([P, PAIRS], F32, "y_sb_%d" % i, tag="tab_%d" % (i % PASSES1))
                 nc.scalar.copy(y_sb[:], y[i][:])
                 for s in range(2):
                     cols = slice(s * HALF, (s + 1) * HALF)

@@ -27,11 +27,11 @@ TILES = H // P
 GROUPS = ((0, 1), (1, 3), (3, 5), (5, 7), (7, 8))
 LAST = len(GROUPS) - 1
 HALVES = S // BANK
-EARLY = 6
-FREE = 0
 HALF = PAIRS // 2
 SCALAR_CASTS = 5
-Y_ORDER = (0, 1) + tuple(range(EARLY, TILES)) + tuple(range(2, EARLY))
+Y_ORDER = (0, 2, 1, 3, 4, 5, 6, 7)
+AHEAD = 8
+ON_GPSIMD = (0, 1)
 
 
 def tile_list_dye_inhibition_kernel(
@@ -180,21 +180,23 @@ def tile_list_dye_inhibition_kernel(
                 for hh in range(HALVES):
                     nc.scalar.copy(h[i][:, hh * BANK : (hh + 1) * BANK], acc[i, hh][:])
 
-        def damping(g, i):
-            u = i % 2
-            tag = None
-            if i >= FREE and g < LAST:
-                tag = ("w_codes_%d_%d", "w_plane_%d_%d")[u] % (PASSES1 - 1, g + 1)
-            x = kept([P, PAIRS], F32, "x_%d" % i, tag="grouped_2_1" if i == 0 else None)
-            nc.vector.tensor_copy(x[:], h[i][:].indirect(pos1_sb[:]))
-            sq = kept([P, PAIRS], F32, "sq_%d" % i, tag=tag or "sq_%d" % u)
-            nc.scalar.activation(sq[:], x[:], ACT.Square)
-            root = kept([P, PAIRS], F32, "root_%d" % i)
-            nc.scalar.activation(root[:], sq[:], ACT.Abs_reciprocal_sqrt, bias=1.0)
-            z = kept([P, PAIRS], BF16, "z_%d" % i)
-            nc.vector.scalar_tensor_tensor(z[:], root[:], gain_sb[:, i : i + 1], root[:], MULT, MULT)
-            b, part = divmod(i, PACK)
-            nc.sync.dma_start(out=z_rows[b][32 * part : 32 * part + 32, :, :], in_=z[:])
+        def damping(tiles):
+            sq = {}
+            for i in tiles:
+                tag = None
+                if i < TILES - 1:
+                    tag = ("w_codes_%d_%d", "w_plane_%d_%d")[i % 2] % (PASSES1 - 1, (i + 1) // 2 + 1)
+                x = kept([P, PAIRS], F32, "x_%d" % i, tag="grouped_2_1" if i == 0 else None)
+                nc.vector.tensor_copy(x[:], h[i][:].indirect(pos1_sb[:]))
+                sq[i] = kept([P, PAIRS], F32, "sq_%d" % i, tag=tag)
+                nc.scalar.activation(sq[i][:], x[:], ACT.Square)
+            for i in tiles:
+                root = kept([P, PAIRS], F32, "root_%d" % i)
+                nc.scalar.activation(root[:], sq[i][:], ACT.Abs_reciprocal_sqrt, bias=1.0)
+                z = kept([P, PAIRS], BF16, "z_%d" % i)
+                nc.vector.scalar_tensor_tensor(z[:], root[:], gain_sb[:, i : i + 1], root[:], MULT, MULT)
+                b, part = divmod(i, PACK)
+                nc.sync.dma_start(out=z_rows[b][32 * part : 32 * part + 32, :, :], in_=z[:])
 
         for a in range(PASSES1):
             gather_words(a)
@@ -217,8 +219,9 @@ def tile_list_dye_inhibition_kernel(
                 scores(g + 1)
             if g + 2 == LAST:
                 scores(LAST)
-            for i in range(*GROUPS[g]):
-                damping(g, i)
+            if g < LAST - 1:
+                damping(range(*GROUPS[g]))
+        damping(range(GROUPS[LAST - 1][0], TILES))
 
         y = {}
         h2 = {}
@@ -229,39 +232,60 @@ def tile_list_dye_inhibition_kernel(
                 h2[i] = picked[:, u, :]
                 nc.vector.tensor_copy(h2[i], h[i][:].indirect(pos2_sb[:]))
 
-        pick_targets((5,), "root_4")
-        pick_targets((0, 1), "root_7")
-        for b in range(PASSES2):
-            tag = "sq_1" if b == 0 else "z_grouped_1"
+        z_codes = {}
+        z_plane = {}
+
+        def quantise_z(b, tag):
             z_grouped = kept([P, PAIRS, PACK], BF16, "z_grouped_%d" % b, tag=tag)
-            nc.scalar.copy(
-                z_grouped[:].rearrange("p (c i) j -> p c j i", i=4),
-                z_rows[b][:].rearrange("p j (c i) -> p c j i", i=4),
-            )
-            z_codes = kept([P, PAIRS], U32, "z_codes_%d" % b)
-            z_plane = kept([P, PAIRS], U8, "z_plane_%d" % b)
-            nc.vector.quantize_mx(
-                out=z_codes[:].bitcast(FP8X4),
-                scales=z_plane[:],
-                in_=z_grouped[:].rearrange("p c j -> p (c j)"),
-            )
-            for i in Y_ORDER:
-                if b == 0:
-                    y[i] = bank(i, "y_%d" % i)
-                nc.tensor.matmul_mx(
-                    out=y[i][:],
-                    lhsT=w2_sb[:, b, :].bitcast(U8)[:, 2 * i * P : 2 * (i + 1) * P].bitcast(FP4X4),
-                    lhsT_scale=w2_plane[:, b, i * P : (i + 1) * P],
-                    rhs=z_codes[:].bitcast(FP8X4),
-                    rhs_scale=z_plane[:],
-                    start=(b == 0),
-                    stop=(b == PASSES2 - 1),
+            z_codes[b] = kept([P, PAIRS], U32, "z_codes_%d" % b)
+            z_plane[b] = kept([P, PAIRS], U8, "z_plane_%d" % b)
+            for s in range(2):
+                cols = slice(s * HALF, (s + 1) * HALF)
+                nc.scalar.copy(
+                    z_grouped[:, cols, :].rearrange("p (c i) j -> p c j i", i=4),
+                    z_rows[b][:, :, cols].rearrange("p j (c i) -> p c j i", i=4),
                 )
-            pick_targets((2, 3) if b == 0 else (4,), tag)
+                nc.vector.quantize_mx(
+                    out=z_codes[b][:, cols].bitcast(FP8X4),
+                    scales=z_plane[b][:, cols],
+                    in_=z_grouped[:, cols, :].rearrange("p c j -> p (c j)"),
+                )
+
+        def stage2_pass(i, b, start):
+            if start:
+                y[i] = bank(i, "y_%d" % i)
+            nc.tensor.matmul_mx(
+                out=y[i][:],
+                lhsT=w2_sb[:, b, :].bitcast(U8)[:, 2 * i * P : 2 * (i + 1) * P].bitcast(FP4X4),
+                lhsT_scale=w2_plane[:, b, i * P : (i + 1) * P],
+                rhs=z_codes[b][:].bitcast(FP8X4),
+                rhs_scale=z_plane[b][:],
+                start=start,
+                stop=not start,
+            )
+
+        pick_targets((0,), "root_3")
+        pick_targets((1,), "root_7")
+        quantise_z(0, "sq_7")
+        for i in Y_ORDER[:AHEAD]:
+            stage2_pass(i, 0, True)
+        pick_targets((2, 3), "z_rows_0")
+        quantise_z(1, None)
+        for i in Y_ORDER[:AHEAD]:
+            stage2_pass(i, 1, False)
+        for i in Y_ORDER[AHEAD:]:
+            stage2_pass(i, 1, True)
+            stage2_pass(i, 0, False)
+        pick_targets((4,), "z_rows_1")
 
         for i in range(TILES):
             res = kept([P, PAIRS], F32, "res_%d" % i, tag="raw_%d_%d" % (i % PASSES1, 2 + i // PASSES1))
-            if i < EARLY:
+            if i in ON_GPSIMD:
+                y_sb = kept([P, PAIRS], F32, "y_sb_%d" % i, tag="grouped_%d_2" % i)
+                nc.scalar.copy(y_sb[:], y[i][:])
+                nc.gpsimd.tensor_tensor(res[:], y_sb[:], h2[i], MULT)
+                nc.sync.dma_start(out=out[i * P : (i + 1) * P, :], in_=res[:])
+            elif i in h2:
                 nc.vector.tensor_tensor(res[:], y[i][:], h2[i], MULT)
                 nc.sync.dma_start(out=out[i * P : (i + 1) * P, :], in_=res[:])
             else:

@@ -29,9 +29,9 @@ LAST = len(GROUPS) - 1
 HALVES = S // BANK
 HALF = PAIRS // 2
 SCALAR_CASTS = 5
-Y_ORDER = (0, 2, 1, 3, 4, 5, 6, 7)
+Y_ORDER = (0, 1, 5, 2, 3, 6, 4, 7)
 AHEAD = 8
-ON_GPSIMD = (0, 1)
+ON_GPSIMD = ()
 
 
 def tile_list_dye_inhibition_kernel(

@@ -291,8 +291,9 @@ def tile_list_dye_inhibition_kernel(
             else:
                 y_sb = kept([P, PAIRS], F32, "y_sb_%d" % i, tag="tab_%d" % (i % PASSES1))
                 nc.scalar.copy(y_sb[:], y[i][:])
-                for s in range(2):
-                    cols = slice(s * HALF, (s + 1) * HALF)
-                    targets = h[i][:].indirect(pos2_sb[:, s * HALF // 16 : (s + 1) * HALF // 16])
-                    nc.vector.tensor_tensor(res[:, cols], targets, y_sb[:, cols], MULT)
-                    nc.sync.dma_start(out=out[i * P : (i + 1) * P, cols], in_=res[:, cols])
+                parts = 2 if i == TILES - 1 else 1
+                for s in range(parts):
+                    first, end = s * PAIRS // parts, (s + 1) * PAIRS // parts
+                    targets = h[i][:].indirect(pos2_sb[:, first // 16 : end // 16])
+                    nc.vector.tensor_tensor(res[:, first:end], targets, y_sb[:, first:end], MULT)
+                    nc.sync.dma_start(out=out[i * P : (i + 1) * P, first:end], in_=res[:, first:end])

@@ -29,8 +29,8 @@ LAST = len(GROUPS) - 1
 HALVES = S // BANK
 HALF = PAIRS // 2
 SCALAR_CASTS = 5
-Y_ORDER = (0, 1, 5, 2, 3, 6, 4, 7)
-AHEAD = 8
+Y_ORDER = (0, 1, 4, 2, 5, 3, 6, 7)
+AHEAD = 6
 ON_GPSIMD = ()
 
 
@@ -192,11 +192,17 @@ def tile_list_dye_inhibition_kernel(
                 nc.scalar.activation(sq[i][:], x[:], ACT.Square)
             for i in tiles:
                 root = kept([P, PAIRS], F32, "root_%d" % i)
-                nc.scalar.activation(root[:], sq[i][:], ACT.Abs_reciprocal_sqrt, bias=1.0)
                 z = kept([P, PAIRS], BF16, "z_%d" % i)
-                nc.vector.scalar_tensor_tensor(z[:], root[:], gain_sb[:, i : i + 1], root[:], MULT, MULT)
                 b, part = divmod(i, PACK)
-                nc.sync.dma_start(out=z_rows[b][32 * part : 32 * part + 32, :, :], in_=z[:])
+                parts = 2 if i == TILES - 1 else 1
+                pieces = [slice(s * PAIRS // parts, (s + 1) * PAIRS // parts) for s in range(parts)]
+                for cols in pieces:
+                    nc.scalar.activation(root[:, cols], sq[i][:, cols], ACT.Abs_reciprocal_sqrt, bias=1.0)
+                for cols in pieces:
+                    nc.vector.scalar_tensor_tensor(
+                        z[:, cols], root[:, cols], gain_sb[:, i : i + 1], root[:, cols], MULT, MULT
+                    )
+                    nc.sync.dma_start(out=z_rows[b][32 * part : 32 * part + 32, :, cols], in_=z[:, cols])
 
         for a in range(PASSES1):
             gather_words(a)
@@ -236,19 +242,19 @@ def tile_list_dye_inhibition_kernel(
         z_plane = {}
 
         def quantise_z(b, tag):
-            z_grouped = kept([P, PAIRS, PACK], BF16, "z_grouped_%d" % b, tag=tag)
             z_codes[b] = kept([P, PAIRS], U32, "z_codes_%d" % b)
             z_plane[b] = kept([P, PAIRS], U8, "z_plane_%d" % b)
             for s in range(2):
                 cols = slice(s * HALF, (s + 1) * HALF)
+                z_grouped = kept([P, HALF, PACK], BF16, "z_grouped_%d_%d" % (b, s), tag=tag[s])
                 nc.scalar.copy(
-                    z_grouped[:, cols, :].rearrange("p (c i) j -> p c j i", i=4),
+                    z_grouped[:].rearrange("p (c i) j -> p c j i", i=4),
                     z_rows[b][:, :, cols].rearrange("p j (c i) -> p c j i", i=4),
                 )
                 nc.vector.quantize_mx(
                     out=z_codes[b][:, cols].bitcast(FP8X4),
                     scales=z_plane[b][:, cols],
-                    in_=z_grouped[:, cols, :].rearrange("p c j -> p (c j)"),
+                    in_=z_grouped[:].rearrange("p c j -> p (c j)"),
                 )
 
         def stage2_pass(i, b, start):
@@ -266,19 +272,18 @@ def tile_list_dye_inhibition_kernel(
 
         pick_targets((0,), "root_3")
         pick_targets((1,), "root_7")
-        quantise_z(0, "sq_7")
+        quantise_z(0, ("sq_7", "x_7"))
         for i in Y_ORDER[:AHEAD]:
             stage2_pass(i, 0, True)
         pick_targets((2, 3), "z_rows_0")
-        quantise_z(1, None)
+        quantise_z(1, (None, None))
         for i in Y_ORDER[:AHEAD]:
             stage2_pass(i, 1, False)
         for i in Y_ORDER[AHEAD:]:
             stage2_pass(i, 1, True)
             stage2_pass(i, 0, False)
-        pick_targets((4,), "z_rows_1")
 
-        for i in range(TILES):
+        for i in Y_ORDER:
             res = kept([P, PAIRS], F32, "res_%d" % i, tag="raw_%d_%d" % (i % PASSES1, 2 + i // PASSES1))
             if i in ON_GPSIMD:
                 y_sb = kept([P, PAIRS], F32, "y_sb_%d" % i, tag="grouped_%d_2" % i)
@@ -289,7 +294,7 @@ def tile_list_dye_inhibition_kernel(
                 nc.vector.tensor_tensor(res[:], y[i][:], h2[i], MULT)
                 nc.sync.dma_start(out=out[i * P : (i + 1) * P, :], in_=res[:])
             else:
-                y_sb = kept([P, PAIRS], F32, "y_sb_%d" % i, tag="tab_%d" % (i % PASSES1))
+                y_sb = kept([P, PAIRS], F32, "y_sb_%d" % i, tag="tab_%d" % (i % PASSES1) if i < 7 else None)
                 nc.scalar.copy(y_sb[:], y[i][:])
                 parts = 2 if i == TILES - 1 else 1
                 for s in range(parts):

@@ -21,6 +21,9 @@ P = 128
 PACK = 4
 K_PASS = P * PACK
 BANK = 512
+BANKS = 8
+QUADRANT = 32
+LIST_ROWS = 16
 PASSES1 = K // K_PASS
 PASSES2 = H // K_PASS
 TILES = H // P
@@ -28,10 +31,10 @@ GROUPS = ((0, 1), (1, 3), (3, 5), (5, 7), (7, 8))
 LAST = len(GROUPS) - 1
 HALVES = S // BANK
 HALF = PAIRS // 2
-SCALAR_CASTS = 5
+SCALAR_ROUNDS = 5
+WALK = 4
 Y_ORDER = (0, 1, 4, 2, 5, 3, 6, 7)
 AHEAD = 6
-ON_GPSIMD = ()
 
 
 def tile_list_dye_inhibition_kernel(
@@ -48,9 +51,9 @@ def tile_list_dye_inhibition_kernel(
         def bank(index, name):
             return psum.tile([P, BANK], F32, name=name, tag="bank%d" % index)
 
-        offs_sb = kept([P, S // 16], U16, "offs_sb")
-        pos1_sb = kept([P, PAIRS // 16], U16, "pos1_sb")
-        pos2_sb = kept([P, PAIRS // 16], U16, "pos2_sb")
+        offs_sb = kept([P, S // LIST_ROWS], U16, "offs_sb")
+        pos1_sb = kept([P, PAIRS // LIST_ROWS], U16, "pos1_sb")
+        pos2_sb = kept([P, PAIRS // LIST_ROWS], U16, "pos2_sb")
         tab_plane = kept([P, T], U8, "tab_plane")
         w2_plane = kept([P, PASSES2, H], U8, "w2_plane")
         gain_rows = kept([P, P], F32, "gain_rows")
@@ -81,9 +84,9 @@ def tile_list_dye_inhibition_kernel(
         load_table(0)
         nc.sync.dma_start(offs_sb[:], offs)
         load_table(1)
-        for q in range(4):
+        for q in range(P // QUADRANT):
             nc.sync.dma_start(
-                out=tab_plane[:].bitcast(I32)[32 * q : 32 * q + 4 * PASSES1, :],
+                out=tab_plane[:].bitcast(I32)[QUADRANT * q : QUADRANT * q + 4 * PASSES1, :],
                 in_=tab_scales.bitcast(I32)[:, 4 * q : 4 * q + 4, :],
             )
         load_w1(0, 0)
@@ -98,13 +101,13 @@ def tile_list_dye_inhibition_kernel(
         nc.sync.dma_start(pos2_sb[:], pos2)
         w2_sb = kept([P, PASSES2, 2 * H // 4], I32, "w2_sb")
         nc.sync.dma_start(out=w2_sb[:], in_=w2_words.bitcast(I32).rearrange("a p c -> p a c"))
-        for q in range(4):
+        for q in range(P // QUADRANT):
             nc.sync.dma_start(
-                out=w2_plane[:].bitcast(I32)[32 * q : 32 * q + 4, :, :],
+                out=w2_plane[:].bitcast(I32)[QUADRANT * q : QUADRANT * q + 4, :, :],
                 in_=w2_scales.bitcast(I32)[:, 4 * q : 4 * q + 4, :].rearrange("a r c -> r a c"),
             )
 
-        gain_ps = bank(7, "gain_ps")
+        gain_ps = bank(BANKS - 1, "gain_ps")
         nc.tensor.transpose(gain_ps[:, 0:P], gain_rows[:], ident[:])
         gain_sb = kept([P, TILES], F32, "gain_sb")
         nc.scalar.copy(gain_sb[:], gain_ps[:, 0:TILES])
@@ -112,7 +115,7 @@ def tile_list_dye_inhibition_kernel(
         v_words = {}
 
         def offs_half(hh):
-            return offs_sb[:, hh * (BANK // 16) : (hh + 1) * (BANK // 16)]
+            return offs_sb[:, hh * (BANK // LIST_ROWS) : (hh + 1) * (BANK // LIST_ROWS)]
 
         def gather_words(a):
             words = kept([P, S], U32, "v_words_%d" % a)
@@ -130,7 +133,6 @@ def tile_list_dye_inhibition_kernel(
         w_codes = {}
         w_plane = {}
         acc = {}
-
         grouped = {}
 
         def width(g):
@@ -138,9 +140,9 @@ def tile_list_dye_inhibition_kernel(
 
         def round_w1(a, g):
             grouped[a, g] = kept([P, width(g), PACK], BF16, "grouped_%d_%d" % (a, g))
-            dst = grouped[a, g][:].rearrange("p (c i) j -> p c j i", i=4)
-            src = raw[a, g][:].rearrange("p j (c i) -> p c j i", i=4)
-            if a > 0 and g * PASSES1 + a >= SCALAR_CASTS:
+            dst = grouped[a, g][:].rearrange("p (c i) j -> p c j i", i=WALK)
+            src = raw[a, g][:].rearrange("p j (c i) -> p c j i", i=WALK)
+            if a > 0 and g * PASSES1 + a >= SCALAR_ROUNDS:
                 nc.vector.tensor_copy(dst, src)
             else:
                 nc.scalar.copy(dst, src)
@@ -159,7 +161,7 @@ def tile_list_dye_inhibition_kernel(
         def stage1_pass(a, g, hh):
             for u, i in enumerate(range(*GROUPS[g])):
                 if a == 0:
-                    acc[i, hh] = bank((HALVES * i + hh) % 8, "acc_%d_%d" % (i, hh))
+                    acc[i, hh] = bank((HALVES * i + hh) % BANKS, "acc_%d_%d" % (i, hh))
                 cols = slice(u * P, (u + 1) * P)
                 nc.tensor.matmul_mx(
                     out=acc[i, hh][:],
@@ -202,7 +204,8 @@ def tile_list_dye_inhibition_kernel(
                     nc.vector.scalar_tensor_tensor(
                         z[:, cols], root[:, cols], gain_sb[:, i : i + 1], root[:, cols], MULT, MULT
                     )
-                    nc.sync.dma_start(out=z_rows[b][32 * part : 32 * part + 32, :, cols], in_=z[:, cols])
+                    rows = z_rows[b][QUADRANT * part : QUADRANT * (part + 1), :, cols]
+                    nc.sync.dma_start(out=rows, in_=z[:, cols])
 
         for a in range(PASSES1):
             gather_words(a)
@@ -241,15 +244,15 @@ def tile_list_dye_inhibition_kernel(
         z_codes = {}
         z_plane = {}
 
-        def quantise_z(b, tag):
+        def quantise_z(b, tags):
             z_codes[b] = kept([P, PAIRS], U32, "z_codes_%d" % b)
             z_plane[b] = kept([P, PAIRS], U8, "z_plane_%d" % b)
             for s in range(2):
                 cols = slice(s * HALF, (s + 1) * HALF)
-                z_grouped = kept([P, HALF, PACK], BF16, "z_grouped_%d_%d" % (b, s), tag=tag[s])
+                z_grouped = kept([P, HALF, PACK], BF16, "z_grouped_%d_%d" % (b, s), tag=tags[s])
                 nc.scalar.copy(
-                    z_grouped[:].rearrange("p (c i) j -> p c j i", i=4),
-                    z_rows[b][:, :, cols].rearrange("p j (c i) -> p c j i", i=4),
+                    z_grouped[:].rearrange("p (c i) j -> p c j i", i=WALK),
+                    z_rows[b][:, :, cols].rearrange("p j (c i) -> p c j i", i=WALK),
                 )
                 nc.vector.quantize_mx(
                     out=z_codes[b][:, cols].bitcast(FP8X4),
@@ -257,17 +260,17 @@ def tile_list_dye_inhibition_kernel(
                     in_=z_grouped[:].rearrange("p c j -> p (c j)"),
                 )
 
-        def stage2_pass(i, b, start):
+        def stage2_pass(i, b, start, cols=slice(0, PAIRS)):
             if start:
                 y[i] = bank(i, "y_%d" % i)
             nc.tensor.matmul_mx(
-                out=y[i][:],
+                out=y[i][:, cols],
                 lhsT=w2_sb[:, b, :].bitcast(U8)[:, 2 * i * P : 2 * (i + 1) * P].bitcast(FP4X4),
                 lhsT_scale=w2_plane[:, b, i * P : (i + 1) * P],
-                rhs=z_codes[b][:].bitcast(FP8X4),
-                rhs_scale=z_plane[b][:],
+                rhs=z_codes[b][:, cols].bitcast(FP8X4),
+                rhs_scale=z_plane[b][:, cols],
                 start=start,
-                stop=not start,
+                stop=not start and cols.stop == PAIRS,
             )
 
         pick_targets((0,), "root_3")
@@ -277,7 +280,9 @@ def tile_list_dye_inhibition_kernel(
             stage2_pass(i, 0, True)
         pick_targets((2, 3), "z_rows_0")
         quantise_z(1, (None, None))
-        for i in Y_ORDER[:AHEAD]:
+        stage2_pass(Y_ORDER[0], 1, False, slice(0, HALF))
+        stage2_pass(Y_ORDER[0], 1, False, slice(HALF, PAIRS))
+        for i in Y_ORDER[1:AHEAD]:
             stage2_pass(i, 1, False)
         for i in Y_ORDER[AHEAD:]:
             stage2_pass(i, 1, True)
@@ -285,20 +290,16 @@ def tile_list_dye_inhibition_kernel(
 
         for i in Y_ORDER:
             res = kept([P, PAIRS], F32, "res_%d" % i, tag="raw_%d_%d" % (i % PASSES1, 2 + i // PASSES1))
-            if i in ON_GPSIMD:
-                y_sb = kept([P, PAIRS], F32, "y_sb_%d" % i, tag="grouped_%d_2" % i)
-                nc.scalar.copy(y_sb[:], y[i][:])
-                nc.gpsimd.tensor_tensor(res[:], y_sb[:], h2[i], MULT)
-                nc.sync.dma_start(out=out[i * P : (i + 1) * P, :], in_=res[:])
-            elif i in h2:
+            if i in h2:
                 nc.vector.tensor_tensor(res[:], y[i][:], h2[i], MULT)
                 nc.sync.dma_start(out=out[i * P : (i + 1) * P, :], in_=res[:])
             else:
-                y_sb = kept([P, PAIRS], F32, "y_sb_%d" % i, tag="tab_%d" % (i % PASSES1) if i < 7 else None)
+                tag = "tab_%d" % (i % PASSES1) if i < TILES - 1 else None
+                y_sb = kept([P, PAIRS], F32, "y_sb_%d" % i, tag=tag)
                 nc.scalar.copy(y_sb[:], y[i][:])
                 parts = 2 if i == TILES - 1 else 1
                 for s in range(parts):
                     first, end = s * PAIRS // parts, (s + 1) * PAIRS // parts
-                    targets = h[i][:].indirect(pos2_sb[:, first // 16 : end // 16])
+                    targets = h[i][:].indirect(pos2_sb[:, first // LIST_ROWS : end // LIST_ROWS])
                     nc.vector.tensor_tensor(res[:, first:end], targets, y_sb[:, first:end], MULT)
                     nc.sync.dma_start(out=out[i * P : (i + 1) * P, first:end], in_=res[:, first:end])

@@ -24,17 +24,20 @@ BANK = 512
 BANKS = 8
 QUADRANT = 32
 LIST_ROWS = 16
+LINE = 16
 PASSES1 = K // K_PASS
 PASSES2 = H // K_PASS
 TILES = H // P
-GROUPS = ((0, 1), (1, 3), (3, 5), (5, 7), (7, 8))
-LAST = len(GROUPS) - 1
 HALVES = S // BANK
 HALF = PAIRS // 2
-SCALAR_ROUNDS = 5
 WALK = 4
-Y_ORDER = (0, 1, 4, 2, 5, 3, 6, 7)
+TINY = 1e-30
+KIB = 1024
+LAST_GATHERS = ((0, 512), (512, 768), (768, 1024))
+BYTES_OF = {F32: 4, I32: 4, U32: 4, BF16: 2, U16: 2, U8: 1}
+Y_ORDER = (7, 2, 0, 3, 1, 4, 5, 6)
 AHEAD = 6
+SPLIT = 2
 
 
 def tile_list_dye_inhibition_kernel(
@@ -42,21 +45,37 @@ def tile_list_dye_inhibition_kernel(
 ):
     nc = tc.nc
     with ExitStack() as ctx:
+        lists = ctx.enter_context(tc.tile_pool(name="lists", bufs=1))
         keep = ctx.enter_context(tc.tile_pool(name="keep", bufs=1))
         psum = ctx.enter_context(tc.psum_pool(name="psum", bufs=1))
 
-        def kept(shape, dtype, name, tag=None):
-            return keep.tile(shape, dtype, name=name, tag=tag or name, align_bytes=64)
+        places = {"end": 0}
+
+        def room(size):
+            first = places["end"]
+            places["end"] = first + (size + 63) // 64 * 64
+            return first
+
+        def kept(shape, dtype, name, on=None, skip=0):
+            if on is None:
+                size = BYTES_OF[dtype]
+                for n in shape[1:]:
+                    size = size * n
+                places[name] = room(size)
+            else:
+                places[name] = places[on] + skip
+            return keep.tile(shape, dtype, name=name, tag=name, align_bytes=64, offset=places[name])
 
         def bank(index, name):
             return psum.tile([P, BANK], F32, name=name, tag="bank%d" % index)
 
-        offs_sb = kept([P, S // LIST_ROWS], U16, "offs_sb")
-        pos1_sb = kept([P, PAIRS // LIST_ROWS], U16, "pos1_sb")
-        pos2_sb = kept([P, PAIRS // LIST_ROWS], U16, "pos2_sb")
+        offs_sb = lists.tile([P, S // LIST_ROWS], U16, name="offs_sb")
+        pos1_sb = lists.tile([P, PAIRS // LIST_ROWS], U16, name="pos1_sb")
+        pos2_sb = lists.tile([P, PAIRS // LIST_ROWS], U16, name="pos2_sb")
         tab_plane = kept([P, T], U8, "tab_plane")
         w2_plane = kept([P, PASSES2, H], U8, "w2_plane")
         gain_rows = kept([P, P], F32, "gain_rows")
+        gain_dealt = kept([P, PASSES2, PACK], F32, "gain_dealt")
         ident = kept([P, P], F32, "ident")
         warm = kept([P, 2], F32, "warm")
 
@@ -71,11 +90,13 @@ def tile_list_dye_inhibition_kernel(
         tab = {}
         raw = {}
 
-        def load_w1(a, g):
-            first, end = GROUPS[g]
-            raw[a, g] = kept([P, PACK, (end - first) * P], F32, "raw_%d_%d" % (a, g))
-            rows = w1[a * K_PASS : (a + 1) * K_PASS, first * P : end * P]
-            nc.sync.dma_start(out=raw[a, g][:], in_=rows.rearrange("(p j) c -> p j c", j=PACK))
+        def load_w1(a, key, first, end, on=None, skip=0):
+            raw[a, key] = kept([P, PACK, end - first], F32, "raw_%d_%s" % (a, key), on, skip)
+            rows = w1[a * K_PASS : (a + 1) * K_PASS, first:end]
+            nc.sync.dma_start(out=raw[a, key][:], in_=rows.rearrange("(p j) c -> p j c", j=PACK))
+
+        def load_group(a, g):
+            load_w1(a, str(g), g * P, (g + 1) * P)
 
         def load_table(a):
             tab[a] = kept([P, T], I32, "tab_%d" % a)
@@ -84,38 +105,51 @@ def tile_list_dye_inhibition_kernel(
         load_table(0)
         nc.sync.dma_start(offs_sb[:], offs)
         load_table(1)
+        nc.sync.dma_start(out=gain_rows[0:PACK, :], in_=gain[0:K_PASS].rearrange("(i q) -> i q", q=P))
+        nc.sync.dma_start(out=gain_dealt[:], in_=gain.rearrange("(b p j) -> p b j", p=P, j=PACK))
         for q in range(P // QUADRANT):
             nc.sync.dma_start(
                 out=tab_plane[:].bitcast(I32)[QUADRANT * q : QUADRANT * q + 4 * PASSES1, :],
                 in_=tab_scales.bitcast(I32)[:, 4 * q : 4 * q + 4, :],
             )
-        load_w1(0, 0)
-        nc.sync.dma_start(out=gain_rows[0:TILES, :], in_=gain.rearrange("(i q) -> i q", q=P))
-        load_w1(1, 0)
-        load_w1(2, 0)
+        load_group(0, 0)
+        load_group(1, 0)
+        load_group(2, 0)
         load_table(2)
         nc.sync.dma_start(pos1_sb[:], pos1)
-        for g in range(1, len(GROUPS)):
+        for g in range(1, PACK):
             for a in range(PASSES1):
-                load_w1(a, g)
+                load_group(a, g)
         nc.sync.dma_start(pos2_sb[:], pos2)
-        w2_sb = kept([P, PASSES2, 2 * H // 4], I32, "w2_sb")
-        nc.sync.dma_start(out=w2_sb[:], in_=w2_words.bitcast(I32).rearrange("a p c -> p a c"))
+        places["three"] = room(6 * KIB)
+        for a in range(PASSES1):
+            for s in range(2):
+                on = "three" if (a, s) == (PASSES1 - 1, 0) else None
+                load_w1(a, "d%d" % s, K_PASS + s * K_PASS // 2, K_PASS + (s + 1) * K_PASS // 2, on, KIB)
         for q in range(P // QUADRANT):
             nc.sync.dma_start(
                 out=w2_plane[:].bitcast(I32)[QUADRANT * q : QUADRANT * q + 4, :, :],
                 in_=w2_scales.bitcast(I32)[:, 4 * q : 4 * q + 4, :].rearrange("a r c -> r a c"),
             )
+        w2_sb = {}
+        for s in (1, 0):
+            w2_sb[s] = kept([P, PASSES2, H // 4], I32, "w2_sb_%d" % s)
+            cols = w2_words.bitcast(I32)[:, :, s * H // 4 : (s + 1) * H // 4]
+            nc.sync.dma_start(out=w2_sb[s][:], in_=cols.rearrange("a p c -> p a c"))
 
         gain_ps = bank(BANKS - 1, "gain_ps")
         nc.tensor.transpose(gain_ps[:, 0:P], gain_rows[:], ident[:])
-        gain_sb = kept([P, TILES], F32, "gain_sb")
-        nc.scalar.copy(gain_sb[:], gain_ps[:, 0:TILES])
+        size = kept([P, TILES], F32, "size")
+        inv_root = kept([P, TILES], F32, "inv_root")
+        inv = kept([P, TILES], F32, "inv")
+        sign = kept([P, PASSES2, PACK], BF16, "sign")
+        nc.scalar.activation(size[:, 0:PACK], gain_ps[:, 0:PACK], ACT.Abs)
+        nc.scalar.activation(size[:, PACK:TILES], gain_dealt[:, 1, :], ACT.Abs)
+        nc.scalar.activation(inv_root[:], size[:], ACT.Abs_reciprocal_sqrt, bias=TINY)
+        nc.scalar.activation(inv[:], inv_root[:], ACT.Square)
+        nc.scalar.activation(sign[:], gain_dealt[:], ACT.Sign)
 
         v_words = {}
-
-        def offs_half(hh):
-            return offs_sb[:, hh * (BANK // LIST_ROWS) : (hh + 1) * (BANK // LIST_ROWS)]
 
         def gather_words(a):
             words = kept([P, S], U32, "v_words_%d" % a)
@@ -123,183 +157,274 @@ def tile_list_dye_inhibition_kernel(
             if a < PASSES1 - 1:
                 nc.vector.tensor_copy(words[:], window.indirect(offs_sb[:]))
             for hh in range(HALVES):
-                v_words[a, hh] = words[:, hh * BANK : (hh + 1) * BANK]
-                if a == PASSES1 - 1:
-                    nc.vector.tensor_copy(v_words[a, hh], window.indirect(offs_half(hh)))
+                v_words[a] = words
+            if a == PASSES1 - 1:
+                for first, end in LAST_GATHERS:
+                    part = offs_sb[:, first // LIST_ROWS : end // LIST_ROWS]
+                    nc.vector.tensor_copy(words[:, first:end], window.indirect(part))
 
         planes = kept([P, S], U8, "v_planes")
         nc.vector.tensor_copy(planes[:], tab_plane[:].indirect(offs_sb[:]))
 
-        w_codes = {}
-        w_plane = {}
-        acc = {}
         grouped = {}
+        weights = {}
+        acc = {}
 
-        def width(g):
-            return (GROUPS[g][1] - GROUPS[g][0]) * P
-
-        def round_w1(a, g):
-            grouped[a, g] = kept([P, width(g), PACK], BF16, "grouped_%d_%d" % (a, g))
-            dst = grouped[a, g][:].rearrange("p (c i) j -> p c j i", i=WALK)
-            src = raw[a, g][:].rearrange("p j (c i) -> p c j i", i=WALK)
-            if a > 0 and g * PASSES1 + a >= SCALAR_ROUNDS:
+        def round_rows(engine, dst, a, g):
+            dst = dst.rearrange("p (c i) j -> p c j i", i=WALK)
+            src = raw[a, str(g)][:].rearrange("p j (c i) -> p c j i", i=WALK)
+            if engine is nc.vector:
                 nc.vector.tensor_copy(dst, src)
             else:
                 nc.scalar.copy(dst, src)
 
-        def quantise_w1(a, g):
-            if (a, g) not in grouped:
-                round_w1(a, g)
-            w_codes[a, g] = kept([P, width(g)], U32, "w_codes_%d_%d" % (a, g))
-            w_plane[a, g] = kept([P, width(g)], U8, "w_plane_%d_%d" % (a, g))
-            nc.vector.quantize_mx(
-                out=w_codes[a, g][:].bitcast(FP8X4),
-                scales=w_plane[a, g][:],
-                in_=grouped[a, g][:].rearrange("p c j -> p (c j)"),
-            )
+        def round_dealt(a, s):
+            if s == 0:
+                grouped[a] = kept([P, K_PASS, PACK], BF16, "grouped_%d_d" % a)
+            dst = grouped[a][:].rearrange("p (t m) j -> p m j t", m=P)[:, s * P // 2 : (s + 1) * P // 2, :, :]
+            src = raw[a, "d%d" % s][:].rearrange("p j (m t) -> p m j t", t=PACK)
+            if s == 1:
+                nc.vector.tensor_copy(dst, src)
+            else:
+                nc.scalar.copy(dst, src)
 
-        def stage1_pass(a, g, hh):
-            for u, i in enumerate(range(*GROUPS[g])):
-                if a == 0:
-                    acc[i, hh] = bank((HALVES * i + hh) % BANKS, "acc_%d_%d" % (i, hh))
-                cols = slice(u * P, (u + 1) * P)
-                nc.tensor.matmul_mx(
-                    out=acc[i, hh][:],
-                    lhsT=w_codes[a, g][:, cols].bitcast(FP8X4),
-                    lhsT_scale=w_plane[a, g][:, cols],
-                    rhs=v_words[a, hh].bitcast(FP8X4),
-                    rhs_scale=planes[4 * a :, hh * BANK : (hh + 1) * BANK],
-                    start=(a == 0),
-                    stop=(a == PASSES1 - 1),
-                )
+        def quantise_w1(rows, name, keys):
+            codes = kept([P, len(keys) * P], U32, "w_codes_" + name)
+            plane = kept([P, len(keys) * P], U8, "w_plane_" + name)
+            nc.vector.quantize_mx(out=codes[:].bitcast(FP8X4), scales=plane[:], in_=rows.rearrange("p c j -> p (c j)"))
+            for u, key in enumerate(keys):
+                weights[key] = (codes[:, u * P : (u + 1) * P], plane[:, u * P : (u + 1) * P])
+
+        def spans(i, a):
+            if (i, a) == (0, PASSES1 - 1):
+                return LAST_GATHERS
+            return [(hh * BANK, (hh + 1) * BANK) for hh in range(HALVES)]
+
+        def stage1(a, tiles):
+            for i in tiles:
+                for first, end in spans(i, a):
+                    hh = first // BANK
+                    if a == 0:
+                        acc[i, hh] = bank((HALVES * i + hh) % BANKS, "acc_%d_%d" % (i, hh))
+                    nc.tensor.matmul_mx(
+                        out=acc[i, hh][:, first - hh * BANK : end - hh * BANK],
+                        lhsT=weights[a, i][0].bitcast(FP8X4),
+                        lhsT_scale=weights[a, i][1],
+                        rhs=v_words[a][:, first:end].bitcast(FP8X4),
+                        rhs_scale=planes[4 * a :, first:end],
+                        start=(a == 0),
+                        stop=(a == PASSES1 - 1 and end % BANK == 0),
+                    )
+
+        rows = {}
+
+        def round_piece(engine, a, i):
+            if i not in rows:
+                rows[i] = kept([P, PASSES1 * P, PACK], BF16, "grouped_%d" % i)
+            round_rows(engine, rows[i][:, a * P : (a + 1) * P, :], a, i)
+
+        def multiply(i):
+            quantise_w1(rows[i][:], str(i), [(a, i) for a in range(PASSES1)])
+            for a in range(PASSES1):
+                stage1(a, [i])
 
         h = {}
-        z_rows = {b: kept([P, PACK, PAIRS], BF16, "z_rows_%d" % b) for b in range(PASSES2)}
+        x = {}
+        sq = {}
+        roots = {0: kept([P, PACK, PAIRS], F32, "roots_0")}
 
-        def scores(g):
-            for i in range(*GROUPS[g]):
-                h[i] = kept([P, S], F32, "h_%d" % i, tag="raw_0_1" if i == 0 else None)
-                for hh in range(HALVES):
-                    nc.scalar.copy(h[i][:, hh * BANK : (hh + 1) * BANK], acc[i, hh][:])
+        def scores(i, on=None):
+            h[i] = kept([P, S], F32, "h_%d" % i, on)
+            for hh in range(HALVES):
+                nc.scalar.copy(h[i][:, hh * BANK : (hh + 1) * BANK], acc[i, hh][:])
 
-        def damping(tiles):
-            sq = {}
-            for i in tiles:
-                tag = None
-                if i < TILES - 1:
-                    tag = ("w_codes_%d_%d", "w_plane_%d_%d")[i % 2] % (PASSES1 - 1, (i + 1) // 2 + 1)
-                x = kept([P, PAIRS], F32, "x_%d" % i, tag="grouped_2_1" if i == 0 else None)
-                nc.vector.tensor_copy(x[:], h[i][:].indirect(pos1_sb[:]))
-                sq[i] = kept([P, PAIRS], F32, "sq_%d" % i, tag=tag)
-                nc.scalar.activation(sq[i][:], x[:], ACT.Square)
-            for i in tiles:
-                root = kept([P, PAIRS], F32, "root_%d" % i)
-                z = kept([P, PAIRS], BF16, "z_%d" % i)
-                b, part = divmod(i, PACK)
-                parts = 2 if i == TILES - 1 else 1
-                pieces = [slice(s * PAIRS // parts, (s + 1) * PAIRS // parts) for s in range(parts)]
-                for cols in pieces:
-                    nc.scalar.activation(root[:, cols], sq[i][:, cols], ACT.Abs_reciprocal_sqrt, bias=1.0)
-                for cols in pieces:
-                    nc.vector.scalar_tensor_tensor(
-                        z[:, cols], root[:, cols], gain_sb[:, i : i + 1], root[:, cols], MULT, MULT
-                    )
-                    rows = z_rows[b][QUADRANT * part : QUADRANT * (part + 1), :, cols]
-                    nc.sync.dma_start(out=rows, in_=z[:, cols])
+        def rivals(i, on=None, skip=0):
+            x[i] = kept([P, PAIRS], F32, "x_%d" % i, on, skip)
+            nc.vector.tensor_copy(x[i][:], h[i][:].indirect(pos1_sb[:]))
+
+        def square(i, on=None, skip=0):
+            sq[i] = kept([P, PAIRS], F32, "sq_%d" % i, on, skip)
+            if i % PACK == PACK - 1:
+                nc.scalar.activation(sq[i][:], x[i][:], ACT.Square)
+            else:
+                nc.gpsimd.tensor_tensor(sq[i][:], x[i][:], x[i][:], MULT)
+
+        def damping(i, on=None, skip=0):
+            gains = inv[:, i : i + 1]
+            if i < PACK:
+                root = kept([P, PAIRS], F32, "root_%d" % i, on, skip)
+                nc.scalar.activation(root[:], sq[i][:], ACT.Abs_reciprocal_sqrt, bias=gains, scale=gains)
+                nc.sync.dma_start(out=roots[0][QUADRANT * i : QUADRANT * (i + 1), :, :], in_=root[:])
+            else:
+                nc.scalar.activation(roots[1][:, i - PACK, :], sq[i][:], ACT.Abs_reciprocal_sqrt, bias=gains, scale=gains)
+
+        sizes = {}
+        z_words = {}
+        z_codes = {b: kept([P, PAIRS], U32, "z_codes_%d" % b) for b in range(PASSES2)}
+        z_plane = {b: kept([P, PAIRS], U8, "z_plane_%d" % b) for b in range(PASSES2)}
+
+        def interleave(b, s, on=None):
+            sizes[b, s] = kept([P, HALF, PACK], BF16, "sizes_%d_%d" % (b, s), on)
+            nc.scalar.activation(
+                sizes[b, s][:].rearrange("p (c i) j -> p c j i", i=WALK),
+                roots[b][:, :, s * HALF : (s + 1) * HALF].rearrange("p j (c i) -> p c j i", i=WALK),
+                ACT.Square,
+            )
+
+        def signs(b, s, on=None):
+            z_words[b, s] = kept([P, HALF, PACK], BF16, "z_words_%d_%d" % (b, s), on)
+            both = sign[:, b, :].unsqueeze(1).to_broadcast([P, HALF, PACK])
+            nc.vector.tensor_tensor(z_words[b, s][:], sizes[b, s][:], both, MULT)
+
+        def quantise_z(b, s):
+            cols = slice(s * HALF, (s + 1) * HALF)
+            nc.vector.quantize_mx(
+                out=z_codes[b][:, cols].bitcast(FP8X4),
+                scales=z_plane[b][:, cols],
+                in_=z_words[b, s][:].rearrange("p c j -> p (c j)"),
+            )
+
+        h2 = {}
+
+        def pick_targets(i, on, skip=0):
+            h2[i] = kept([P, PAIRS], F32, "h2_%d" % i, on, skip)
+            nc.vector.tensor_copy(h2[i][:], h[i][:].indirect(pos2_sb[:]))
+
+        def deal_w2():
+            words = kept([P, PASSES2, K_PASS], U16, "w2_dealt_words", "grouped_2_d")
+            plane = kept([P, PASSES2, K_PASS], U8, "w2_dealt_plane", "grouped_2_d", 2 * KIB)
+            n = LINE // 2
+            nc.vector.tensor_copy(
+                plane[:].rearrange("p b (t c i) -> p b c t i", t=PACK, i=LINE),
+                w2_plane[:, :, K_PASS:H].rearrange("p b (c i t) -> p b c t i", t=PACK, i=LINE),
+            )
+            nc.vector.tensor_copy(
+                words[:].rearrange("p b (t c i) -> p b c t i", t=PACK, i=n),
+                w2_sb[1][:].bitcast(U16).rearrange("p b (c i t) -> p b c t i", t=PACK, i=n),
+            )
+            return words, plane
 
         for a in range(PASSES1):
             gather_words(a)
-
-        def prepare(g):
+        for i in range(2):
             for a in range(PASSES1):
-                quantise_w1(a, g)
-                for hh in range(HALVES):
-                    stage1_pass(a, g, hh)
-
-        prepare(0)
-        prepare(1)
-        scores(0)
-        for g in range(len(GROUPS)):
-            if g + 2 <= LAST:
-                prepare(g + 2)
-            if g + 3 <= LAST:
-                round_w1(0, g + 3)
-            if g + 1 < LAST:
-                scores(g + 1)
-            if g + 2 == LAST:
-                scores(LAST)
-            if g < LAST - 1:
-                damping(range(*GROUPS[g]))
-        damping(range(GROUPS[LAST - 1][0], TILES))
+                first = kept([P, P, PACK], BF16, "grouped_%d_%d" % (a, i))
+                round_rows(nc.scalar, first[:], a, i)
+                quantise_w1(first[:], "%d_%d" % (a, i), [(a, i)])
+                stage1(a, [i])
+        scores(0, "raw_1_1")
+        for a in range(PASSES1):
+            round_piece(nc.vector, a, 2)
+        multiply(2)
+        rivals(0, "grouped_2")
+        round_piece(nc.scalar, 0, 3)
+        round_piece(nc.scalar, 1, 3)
+        round_piece(nc.vector, 2, 3)
+        scores(1, "raw_0_3")
+        multiply(3)
+        rivals(1, "grouped_3")
+        square(0, "raw_2_3")
+        dealt = range(PACK, TILES)
+        round_dealt(0, 0)
+        round_dealt(0, 1)
+        scores(2, "raw_0_d0")
+        quantise_w1(grouped[0][:], "0_d", [(0, i) for i in dealt])
+        stage1(0, dealt)
+        round_dealt(1, 0)
+        round_dealt(1, 1)
+        rivals(2, "raw_1_d1")
+        square(1, "grouped_0_d")
+        damping(0, "grouped_0_d", 2 * KIB)
+        scores(3, "raw_1_d0")
+        quantise_w1(grouped[1][:], "1_d", [(1, i) for i in dealt])
+        stage1(1, dealt)
+        rivals(3, "grouped_1_d")
+        square(2)
+        round_dealt(2, 0)
+        round_dealt(2, 1)
+        damping(1, "three")
+        square(3, "three", 4 * KIB)
+        damping(2, "three", 2 * KIB)
+        damping(3)
+        quantise_w1(grouped[2][:, 0 : 2 * P, :], "2_d0", [(2, 4), (2, 5)])
+        quantise_w1(grouped[2][:, 2 * P :, :], "2_d1", [(2, 6), (2, 7)])
+        stage1(2, dealt)
+        dealt_words, dealt_plane = deal_w2()
+        for i in dealt:
+            scores(i)
+            rivals(i, "w2_sb_1" if i == PACK else None)
+            if i < TILES - 1:
+                square(i)
+        pick_targets(7, None)
+        interleave(0, 0)
+        interleave(0, 1)
+        signs(0, 0, "x_6")
+        signs(0, 1)
+        quantise_z(0, 0)
+        quantise_z(0, 1)
+        pick_targets(0, "z_words_0_0")
+        pick_targets(1, "z_words_0_1")
+        roots[1] = kept([P, PACK, PAIRS], F32, "roots_1", "roots_0")
+        damping(4)
+        damping(5)
+        square(7, "sq_4")
+        damping(6)
+        damping(7)
 
         y = {}
-        h2 = {}
 
-        def pick_targets(tiles, tag):
-            picked = kept([P, len(tiles), PAIRS], F32, "h2_%d" % tiles[0], tag=tag)
-            for u, i in enumerate(tiles):
-                h2[i] = picked[:, u, :]
-                nc.vector.tensor_copy(h2[i], h[i][:].indirect(pos2_sb[:]))
-
-        z_codes = {}
-        z_plane = {}
-
-        def quantise_z(b, tags):
-            z_codes[b] = kept([P, PAIRS], U32, "z_codes_%d" % b)
-            z_plane[b] = kept([P, PAIRS], U8, "z_plane_%d" % b)
-            for s in range(2):
-                cols = slice(s * HALF, (s + 1) * HALF)
-                z_grouped = kept([P, HALF, PACK], BF16, "z_grouped_%d_%d" % (b, s), tag=tags[s])
-                nc.scalar.copy(
-                    z_grouped[:].rearrange("p (c i) j -> p c j i", i=WALK),
-                    z_rows[b][:, :, cols].rearrange("p j (c i) -> p c j i", i=WALK),
-                )
-                nc.vector.quantize_mx(
-                    out=z_codes[b][:, cols].bitcast(FP8X4),
-                    scales=z_plane[b][:, cols],
-                    in_=z_grouped[:].rearrange("p c j -> p (c j)"),
-                )
-
-        def stage2_pass(i, b, start, cols=slice(0, PAIRS)):
+        def stage2(i, b, cols=slice(0, PAIRS)):
+            start = i not in y
             if start:
                 y[i] = bank(i, "y_%d" % i)
+            if i < PACK:
+                words = w2_sb[0][:, b, :].bitcast(U8)[:, 2 * i * P : 2 * (i + 1) * P]
+                plane = w2_plane[:, b, i * P : (i + 1) * P]
+            else:
+                t = i - PACK
+                words = dealt_words[:, b, t * P : (t + 1) * P].bitcast(U8)
+                plane = dealt_plane[:, b, t * P : (t + 1) * P]
             nc.tensor.matmul_mx(
                 out=y[i][:, cols],
-                lhsT=w2_sb[:, b, :].bitcast(U8)[:, 2 * i * P : 2 * (i + 1) * P].bitcast(FP4X4),
-                lhsT_scale=w2_plane[:, b, i * P : (i + 1) * P],
+                lhsT=words.bitcast(FP4X4),
+                lhsT_scale=plane,
                 rhs=z_codes[b][:, cols].bitcast(FP8X4),
                 rhs_scale=z_plane[b][:, cols],
                 start=start,
-                stop=not start and cols.stop == PAIRS,
+                stop=(not start and cols.stop == PAIRS),
             )
 
-        pick_targets((0,), "root_3")
-        pick_targets((1,), "root_7")
-        quantise_z(0, ("sq_7", "x_7"))
         for i in Y_ORDER[:AHEAD]:
-            stage2_pass(i, 0, True)
-        pick_targets((2, 3), "z_rows_0")
-        quantise_z(1, (None, None))
-        stage2_pass(Y_ORDER[0], 1, False, slice(0, HALF))
-        stage2_pass(Y_ORDER[0], 1, False, slice(HALF, PAIRS))
-        for i in Y_ORDER[1:AHEAD]:
-            stage2_pass(i, 1, False)
+            stage2(i, 0)
+        interleave(1, 0)
+        interleave(1, 1)
+        for s in range(2):
+            signs(1, s)
+            quantise_z(1, s)
+            for i in Y_ORDER[:SPLIT]:
+                stage2(i, 1, slice(s * HALF, (s + 1) * HALF))
+        for i in Y_ORDER[SPLIT:AHEAD]:
+            stage2(i, 1)
         for i in Y_ORDER[AHEAD:]:
-            stage2_pass(i, 1, True)
-            stage2_pass(i, 0, False)
+            stage2(i, 1)
+            stage2(i, 0)
 
+        results = [kept([P, PACK, PAIRS], F32, "res_%d" % b, None if b == 0 else "tab_2") for b in range(PASSES2)]
+        copies = [kept([P, PACK, PAIRS], F32, "y_sb_%d" % b, "tab_%d" % b) for b in range(PASSES2)]
+        dealt_out = out[K_PASS:H, :].rearrange("(p t) m -> p t m", t=PACK)
         for i in Y_ORDER:
-            res = kept([P, PAIRS], F32, "res_%d" % i, tag="raw_%d_%d" % (i % PASSES1, 2 + i // PASSES1))
+            b, u = divmod(i, PACK)
+            res = results[b][:, u, :]
+            rows = out[i * P : (i + 1) * P, :] if b == 0 else dealt_out[:, u, :]
             if i in h2:
-                nc.vector.tensor_tensor(res[:], y[i][:], h2[i], MULT)
-                nc.sync.dma_start(out=out[i * P : (i + 1) * P, :], in_=res[:])
+                nc.vector.tensor_tensor(res, y[i][:], h2[i][:], MULT)
+                nc.sync.dma_start(out=rows, in_=res)
             else:
-                tag = "tab_%d" % (i % PASSES1) if i < TILES - 1 else None
-                y_sb = kept([P, PAIRS], F32, "y_sb_%d" % i, tag=tag)
-                nc.scalar.copy(y_sb[:], y[i][:])
-                parts = 2 if i == TILES - 1 else 1
+                y_sb = copies[b][:, u, :]
+                nc.scalar.copy(y_sb, y[i][:])
+                parts = 2 if i == Y_ORDER[-1] else 1
                 for s in range(parts):
                     first, end = s * PAIRS // parts, (s + 1) * PAIRS // parts
                     targets = h[i][:].indirect(pos2_sb[:, first // LIST_ROWS : end // LIST_ROWS])
                     nc.vector.tensor_tensor(res[:, first:end], targets, y_sb[:, first:end], MULT)
-                    nc.sync.dma_start(out=out[i * P : (i + 1) * P, first:end], in_=res[:, first:end])
+                    nc.sync.dma_start(out=rows[:, first:end], in_=res[:, first:end])

@@ -35,8 +35,10 @@ TINY = 1e-30
 KIB = 1024
 LAST_GATHERS = ((0, 512), (512, 768), (768, 1024))
 BYTES_OF = {F32: 4, I32: 4, U32: 4, BF16: 2, U16: 2, U8: 1}
-Y_ORDER = (7, 2, 0, 3, 1, 4, 5, 6)
-AHEAD = 6
+Y_ORDER = (7, 2, 0, 1, 3, 4, 5, 6)
+OUT_ORDER = (7, 0, 1, 2, 3, 4, 5, 6)
+AHEAD = 4
+Z_PIECES = (((0, 256), (256, 512)), ((0, 256), (256, 384), (384, 512)))
 SPLIT = 2
 
 
@@ -96,6 +98,8 @@ def tile_list_dye_inhibition_kernel(
             nc.sync.dma_start(out=raw[a, key][:], in_=rows.rearrange("(p j) c -> p j c", j=PACK))
 
         def load_group(a, g):
+            if g == PACK - 1 and a != 1:
+                places["ahead_%d" % a] = room((2 - a // 2) * KIB)
             load_w1(a, str(g), g * P, (g + 1) * P)
 
         def load_table(a):
@@ -120,12 +124,13 @@ def tile_list_dye_inhibition_kernel(
         for g in range(1, PACK):
             for a in range(PASSES1):
                 load_group(a, g)
+        room(KIB)
         nc.sync.dma_start(pos2_sb[:], pos2)
-        places["three"] = room(6 * KIB)
         for a in range(PASSES1):
             for s in range(2):
-                on = "three" if (a, s) == (PASSES1 - 1, 0) else None
-                load_w1(a, "d%d" % s, K_PASS + s * K_PASS // 2, K_PASS + (s + 1) * K_PASS // 2, on, KIB)
+                if (a, s) == (1, 0):
+                    places["ahead_d"] = room(2 * KIB)
+                load_w1(a, "d%d" % s, K_PASS + s * K_PASS // 2, K_PASS + (s + 1) * K_PASS // 2)
         for q in range(P // QUADRANT):
             nc.sync.dma_start(
                 out=w2_plane[:].bitcast(I32)[QUADRANT * q : QUADRANT * q + 4, :, :],
@@ -244,7 +249,7 @@ def tile_list_dye_inhibition_kernel(
 
         def square(i, on=None, skip=0):
             sq[i] = kept([P, PAIRS], F32, "sq_%d" % i, on, skip)
-            if i % PACK == PACK - 1:
+            if i == PACK - 1:
                 nc.scalar.activation(sq[i][:], x[i][:], ACT.Square)
             else:
                 nc.gpsimd.tensor_tensor(sq[i][:], x[i][:], x[i][:], MULT)
@@ -256,7 +261,12 @@ def tile_list_dye_inhibition_kernel(
                 nc.scalar.activation(root[:], sq[i][:], ACT.Abs_reciprocal_sqrt, bias=gains, scale=gains)
                 nc.sync.dma_start(out=roots[0][QUADRANT * i : QUADRANT * (i + 1), :, :], in_=root[:])
             else:
-                nc.scalar.activation(roots[1][:, i - PACK, :], sq[i][:], ACT.Abs_reciprocal_sqrt, bias=gains, scale=gains)
+                parts = 2 if i == TILES - 1 else 1
+                for s in range(parts):
+                    cols = slice(s * PAIRS // parts, (s + 1) * PAIRS // parts)
+                    nc.scalar.activation(
+                        roots[1][:, i - PACK, cols], sq[i][:, cols], ACT.Abs_reciprocal_sqrt, bias=gains, scale=gains
+                    )
 
         sizes = {}
         z_words = {}
@@ -264,20 +274,24 @@ def tile_list_dye_inhibition_kernel(
         z_plane = {b: kept([P, PAIRS], U8, "z_plane_%d" % b) for b in range(PASSES2)}
 
         def interleave(b, s, on=None):
-            sizes[b, s] = kept([P, HALF, PACK], BF16, "sizes_%d_%d" % (b, s), on)
+            first, end = Z_PIECES[b][s]
+            sizes[b, s] = kept([P, end - first, PACK], BF16, "sizes_%d_%d" % (b, s), on)
             nc.scalar.activation(
                 sizes[b, s][:].rearrange("p (c i) j -> p c j i", i=WALK),
-                roots[b][:, :, s * HALF : (s + 1) * HALF].rearrange("p j (c i) -> p c j i", i=WALK),
+                roots[b][:, :, first:end].rearrange("p j (c i) -> p c j i", i=WALK),
                 ACT.Square,
             )
 
         def signs(b, s, on=None):
-            z_words[b, s] = kept([P, HALF, PACK], BF16, "z_words_%d_%d" % (b, s), on)
-            both = sign[:, b, :].unsqueeze(1).to_broadcast([P, HALF, PACK])
+            first, end = Z_PIECES[b][s]
+            z_words[b, s] = kept([P, end - first, PACK], BF16, "z_words_%d_%d" % (b, s), on)
+            if (b, s) == (1, 1):
+                room(KIB)
+            both = sign[:, b, :].unsqueeze(1).to_broadcast([P, end - first, PACK])
             nc.vector.tensor_tensor(z_words[b, s][:], sizes[b, s][:], both, MULT)
 
         def quantise_z(b, s):
-            cols = slice(s * HALF, (s + 1) * HALF)
+            cols = slice(*Z_PIECES[b][s])
             nc.vector.quantize_mx(
                 out=z_codes[b][:, cols].bitcast(FP8X4),
                 scales=z_plane[b][:, cols],
@@ -316,35 +330,35 @@ def tile_list_dye_inhibition_kernel(
         for a in range(PASSES1):
             round_piece(nc.vector, a, 2)
         multiply(2)
-        rivals(0, "grouped_2")
+        rivals(0, "raw_2_2")
         round_piece(nc.scalar, 0, 3)
         round_piece(nc.scalar, 1, 3)
         round_piece(nc.vector, 2, 3)
-        scores(1, "raw_0_3")
+        scores(1, "ahead_0")
         multiply(3)
-        rivals(1, "grouped_3")
-        square(0, "raw_2_3")
+        rivals(1, "ahead_2")
+        square(0, "ahead_2", 2 * KIB)
         dealt = range(PACK, TILES)
         round_dealt(0, 0)
         round_dealt(0, 1)
-        scores(2, "raw_0_d0")
+        scores(2)
         quantise_w1(grouped[0][:], "0_d", [(0, i) for i in dealt])
         stage1(0, dealt)
         round_dealt(1, 0)
         round_dealt(1, 1)
-        rivals(2, "raw_1_d1")
+        rivals(2, "raw_1_d0", 2 * KIB)
         square(1, "grouped_0_d")
         damping(0, "grouped_0_d", 2 * KIB)
-        scores(3, "raw_1_d0")
+        scores(3, "ahead_d")
         quantise_w1(grouped[1][:], "1_d", [(1, i) for i in dealt])
         stage1(1, dealt)
-        rivals(3, "grouped_1_d")
+        rivals(3, "raw_1_d1", 2 * KIB)
         square(2)
         round_dealt(2, 0)
         round_dealt(2, 1)
-        damping(1, "three")
-        square(3, "three", 4 * KIB)
-        damping(2, "three", 2 * KIB)
+        damping(1)
+        square(3)
+        damping(2)
         damping(3)
         quantise_w1(grouped[2][:, 0 : 2 * P, :], "2_d0", [(2, 4), (2, 5)])
         quantise_w1(grouped[2][:, 2 * P :, :], "2_d1", [(2, 6), (2, 7)])
@@ -353,23 +367,18 @@ def tile_list_dye_inhibition_kernel(
         for i in dealt:
             scores(i)
             rivals(i, "w2_sb_1" if i == PACK else None)
-            if i < TILES - 1:
-                square(i)
+            square(i)
         pick_targets(7, None)
+        pick_targets(0, "x_6")
         interleave(0, 0)
         interleave(0, 1)
-        signs(0, 0, "x_6")
+        signs(0, 0, "x_7")
         signs(0, 1)
         quantise_z(0, 0)
         quantise_z(0, 1)
-        pick_targets(0, "z_words_0_0")
-        pick_targets(1, "z_words_0_1")
         roots[1] = kept([P, PACK, PAIRS], F32, "roots_1", "roots_0")
-        damping(4)
-        damping(5)
-        square(7, "sq_4")
-        damping(6)
-        damping(7)
+        for i in dealt:
+            damping(i)
 
         y = {}
 
@@ -396,13 +405,17 @@ def tile_list_dye_inhibition_kernel(
 
         for i in Y_ORDER[:AHEAD]:
             stage2(i, 0)
-        interleave(1, 0)
-        interleave(1, 1)
-        for s in range(2):
-            signs(1, s)
+        last = range(len(Z_PIECES[1]))
+        for s in last:
+            interleave(1, s)
+        signs(1, 0)
+        for s in last:
+            if s + 1 in last:
+                signs(1, s + 1)
             quantise_z(1, s)
             for i in Y_ORDER[:SPLIT]:
-                stage2(i, 1, slice(s * HALF, (s + 1) * HALF))
+                stage2(i, 1, slice(*Z_PIECES[1][s]))
+        pick_targets(1, "z_words_1_1")
         for i in Y_ORDER[SPLIT:AHEAD]:
             stage2(i, 1)
         for i in Y_ORDER[AHEAD:]:
@@ -412,7 +425,7 @@ def tile_list_dye_inhibition_kernel(
         results = [kept([P, PACK, PAIRS], F32, "res_%d" % b, None if b == 0 else "tab_2") for b in range(PASSES2)]
         copies = [kept([P, PACK, PAIRS], F32, "y_sb_%d" % b, "tab_%d" % b) for b in range(PASSES2)]
         dealt_out = out[K_PASS:H, :].rearrange("(p t) m -> p t m", t=PACK)
-        for i in Y_ORDER:
+        for i in OUT_ORDER:
             b, u = divmod(i, PACK)
             res = results[b][:, u, :]
             rows = out[i * P : (i + 1) * P, :] if b == 0 else dealt_out[:, u, :]
@@ -422,7 +435,7 @@ def tile_list_dye_inhibition_kernel(
             else:
                 y_sb = copies[b][:, u, :]
                 nc.scalar.copy(y_sb, y[i][:])
-                parts = 2 if i == Y_ORDER[-1] else 1
+                parts = 2 if i == OUT_ORDER[-1] else 1
                 for s in range(parts):
                     first, end = s * PAIRS // parts, (s + 1) * PAIRS // parts
                     targets = h[i][:].indirect(pos2_sb[:, first // LIST_ROWS : end // LIST_ROWS])

@@ -37,9 +37,9 @@ LAST_GATHERS = ((0, 512), (512, 768), (768, 1024))
 BYTES_OF = {F32: 4, I32: 4, U32: 4, BF16: 2, U16: 2, U8: 1}
 Y_ORDER = (7, 2, 0, 1, 3, 4, 5, 6)
 OUT_ORDER = (7, 0, 1, 2, 3, 4, 5, 6)
-AHEAD = 4
+AHEAD = 3
 Z_PIECES = (((0, 256), (256, 512)), ((0, 256), (256, 384), (384, 512)))
-SPLIT = 2
+SPLIT = 1
 
 
 def tile_list_dye_inhibition_kernel(
@@ -282,9 +282,9 @@ def tile_list_dye_inhibition_kernel(
                 ACT.Square,
             )
 
-        def signs(b, s, on=None):
+        def signs(b, s, on=None, skip=0):
             first, end = Z_PIECES[b][s]
-            z_words[b, s] = kept([P, end - first, PACK], BF16, "z_words_%d_%d" % (b, s), on)
+            z_words[b, s] = kept([P, end - first, PACK], BF16, "z_words_%d_%d" % (b, s), on, skip)
             if (b, s) == (1, 1):
                 room(KIB)
             both = sign[:, b, :].unsqueeze(1).to_broadcast([P, end - first, PACK])
@@ -364,15 +364,16 @@ def tile_list_dye_inhibition_kernel(
         quantise_w1(grouped[2][:, 2 * P :, :], "2_d1", [(2, 6), (2, 7)])
         stage1(2, dealt)
         dealt_words, dealt_plane = deal_w2()
+        places["pair"] = room(4 * KIB)
         for i in dealt:
             scores(i)
-            rivals(i, "w2_sb_1" if i == PACK else None)
+            rivals(i, {4: "w2_sb_1", 6: "pair"}.get(i), KIB if i == 6 else 0)
             square(i)
         pick_targets(7, None)
-        pick_targets(0, "x_6")
+        pick_targets(0, "pair")
         interleave(0, 0)
         interleave(0, 1)
-        signs(0, 0, "x_7")
+        signs(0, 0, "pair", 2 * KIB)
         signs(0, 1)
         quantise_z(0, 0)
         quantise_z(0, 1)

@@ -137,10 +137,13 @@ def tile_list_dye_inhibition_kernel(
                 in_=w2_scales.bitcast(I32)[:, 4 * q : 4 * q + 4, :].rearrange("a r c -> r a c"),
             )
         w2_sb = {}
-        for s in (1, 0):
-            w2_sb[s] = kept([P, PASSES2, H // 4], I32, "w2_sb_%d" % s)
+
+        def load_w2(s, on=None):
+            w2_sb[s] = kept([P, PASSES2, H // 4], I32, "w2_sb_%d" % s, on)
             cols = w2_words.bitcast(I32)[:, :, s * H // 4 : (s + 1) * H // 4]
             nc.sync.dma_start(out=w2_sb[s][:], in_=cols.rearrange("a p c -> p a c"))
+
+        load_w2(1)
 
         gain_ps = bank(BANKS - 1, "gain_ps")
         nc.tensor.transpose(gain_ps[:, 0:P], gain_rows[:], ident[:])
@@ -257,16 +260,15 @@ def tile_list_dye_inhibition_kernel(
         def damping(i, on=None, skip=0):
             gains = inv[:, i : i + 1]
             if i < PACK:
-                root = kept([P, PAIRS], F32, "root_%d" % i, on, skip)
-                nc.scalar.activation(root[:], sq[i][:], ACT.Abs_reciprocal_sqrt, bias=gains, scale=gains)
-                nc.sync.dma_start(out=roots[0][QUADRANT * i : QUADRANT * (i + 1), :, :], in_=root[:])
+                root = kept([P, PAIRS], F32, "root_%d" % i, on, skip)[:]
             else:
-                parts = 2 if i == TILES - 1 else 1
-                for s in range(parts):
-                    cols = slice(s * PAIRS // parts, (s + 1) * PAIRS // parts)
-                    nc.scalar.activation(
-                        roots[1][:, i - PACK, cols], sq[i][:, cols], ACT.Abs_reciprocal_sqrt, bias=gains, scale=gains
-                    )
+                root = roots[1][:, i - PACK, :]
+            parts = 2 if i % PACK == PACK - 1 else 1
+            for s in range(parts):
+                cols = slice(s * PAIRS // parts, (s + 1) * PAIRS // parts)
+                nc.scalar.activation(root[:, cols], sq[i][:, cols], ACT.Abs_reciprocal_sqrt, bias=gains, scale=gains)
+                if i < PACK:
+                    nc.sync.dma_start(out=roots[0][QUADRANT * i : QUADRANT * (i + 1), :, cols], in_=root[:, cols])
 
         sizes = {}
         z_words = {}
@@ -360,6 +362,7 @@ def tile_list_dye_inhibition_kernel(
         square(3)
         damping(2)
         damping(3)
+        load_w2(0, "root_3")
         quantise_w1(grouped[2][:, 0 : 2 * P, :], "2_d0", [(2, 4), (2, 5)])
         quantise_w1(grouped[2][:, 2 * P :, :], "2_d1", [(2, 6), (2, 7)])
         stage1(2, dealt)

@@ -239,7 +239,8 @@ def tile_list_dye_inhibition_kernel(
         h = {}
         x = {}
         sq = {}
-        roots = {0: kept([P, PACK, PAIRS], F32, "roots_0")}
+        places["roots"] = room(8 * KIB)
+        moved = {0: kept([P, PACK, HALF], F32, "moved_0", "roots")}
 
         def scores(i, on=None):
             h[i] = kept([P, S], F32, "h_%d" % i, on)
@@ -257,18 +258,22 @@ def tile_list_dye_inhibition_kernel(
             else:
                 nc.gpsimd.tensor_tensor(sq[i][:], x[i][:], x[i][:], MULT)
 
+        root = {}
+        halves = (slice(0, HALF), slice(HALF, PAIRS))
+
+        def move(i, s):
+            nc.sync.dma_start(out=moved[s][QUADRANT * i : QUADRANT * (i + 1), :, :], in_=root[i][:, halves[s]])
+
         def damping(i, on=None, skip=0):
             gains = inv[:, i : i + 1]
             if i < PACK:
-                root = kept([P, PAIRS], F32, "root_%d" % i, on, skip)[:]
+                root[i] = kept([P, PAIRS], F32, "root_%d" % i, on, skip)[:]
             else:
-                root = roots[1][:, i - PACK, :]
-            parts = 2 if i % PACK == PACK - 1 else 1
-            for s in range(parts):
-                cols = slice(s * PAIRS // parts, (s + 1) * PAIRS // parts)
-                nc.scalar.activation(root[:, cols], sq[i][:, cols], ACT.Abs_reciprocal_sqrt, bias=gains, scale=gains)
-                if i < PACK:
-                    nc.sync.dma_start(out=roots[0][QUADRANT * i : QUADRANT * (i + 1), :, cols], in_=root[:, cols])
+                root[i] = dealt_roots[:, i - PACK, :]
+            for cols in halves if i % PACK == PACK - 1 else [slice(0, PAIRS)]:
+                nc.scalar.activation(root[i][:, cols], sq[i][:, cols], ACT.Abs_reciprocal_sqrt, bias=gains, scale=gains)
+            if i < PACK:
+                move(i, 0)
 
         sizes = {}
         z_words = {}
@@ -280,7 +285,7 @@ def tile_list_dye_inhibition_kernel(
             sizes[b, s] = kept([P, end - first, PACK], BF16, "sizes_%d_%d" % (b, s), on)
             nc.scalar.activation(
                 sizes[b, s][:].rearrange("p (c i) j -> p c j i", i=WALK),
-                roots[b][:, :, first:end].rearrange("p j (c i) -> p c j i", i=WALK),
+                (moved[s][:] if b == 0 else dealt_roots[:, :, first:end]).rearrange("p j (c i) -> p c j i", i=WALK),
                 ACT.Square,
             )
 
@@ -359,9 +364,12 @@ def tile_list_dye_inhibition_kernel(
         round_dealt(2, 0)
         round_dealt(2, 1)
         damping(1)
-        square(3)
+        square(3, "roots", 4 * KIB)
         damping(2)
         damping(3)
+        moved[1] = kept([P, PACK, HALF], F32, "moved_1", "roots", 4 * KIB)
+        for i in range(PACK):
+            move(i, 1)
         load_w2(0, "root_3")
         quantise_w1(grouped[2][:, 0 : 2 * P, :], "2_d0", [(2, 4), (2, 5)])
         quantise_w1(grouped[2][:, 2 * P :, :], "2_d1", [(2, 6), (2, 7)])
@@ -380,7 +388,7 @@ def tile_list_dye_inhibition_kernel(
         signs(0, 1)
         quantise_z(0, 0)
         quantise_z(0, 1)
-        roots[1] = kept([P, PACK, PAIRS], F32, "roots_1", "roots_0")
+        dealt_roots = kept([P, PACK, PAIRS], F32, "dealt_roots", "roots")
         for i in dealt:
             damping(i)
 

@@ -76,8 +76,7 @@ def tile_list_dye_inhibition_kernel(
         pos2_sb = lists.tile([P, PAIRS // LIST_ROWS], U16, name="pos2_sb")
         tab_plane = kept([P, T], U8, "tab_plane")
         w2_plane = kept([P, PASSES2, H], U8, "w2_plane")
-        gain_rows = kept([P, P], F32, "gain_rows")
-        gain_dealt = kept([P, PASSES2, PACK], F32, "gain_dealt")
+        gain_rows = kept([P, K_PASS], F32, "gain_rows")
         ident = kept([P, P], F32, "ident")
         warm = kept([P, 2], F32, "warm")
 
@@ -109,8 +108,7 @@ def tile_list_dye_inhibition_kernel(
         load_table(0)
         nc.sync.dma_start(offs_sb[:], offs)
         load_table(1)
-        nc.sync.dma_start(out=gain_rows[0:PACK, :], in_=gain[0:K_PASS].rearrange("(i q) -> i q", q=P))
-        nc.sync.dma_start(out=gain_dealt[:], in_=gain.rearrange("(b p j) -> p b j", p=P, j=PACK))
+        nc.sync.dma_start(out=gain_rows[0:PASSES2, :], in_=gain.rearrange("(b r) -> b r", r=K_PASS))
         for q in range(P // QUADRANT):
             nc.sync.dma_start(
                 out=tab_plane[:].bitcast(I32)[QUADRANT * q : QUADRANT * q + 4 * PASSES1, :],
@@ -118,8 +116,8 @@ def tile_list_dye_inhibition_kernel(
             )
         load_group(0, 0)
         load_group(1, 0)
-        load_group(2, 0)
         load_table(2)
+        load_group(2, 0)
         nc.sync.dma_start(pos1_sb[:], pos1)
         for g in range(1, PACK):
             for a in range(PASSES1):
@@ -145,31 +143,36 @@ def tile_list_dye_inhibition_kernel(
 
         load_w2(1)
 
-        gain_ps = bank(BANKS - 1, "gain_ps")
-        nc.tensor.transpose(gain_ps[:, 0:P], gain_rows[:], ident[:])
+        natural = bank(BANKS - 2, "gain_natural")
+        by_word = bank(BANKS - 1, "gain_by_word")
+        for j in range(PACK):
+            nc.tensor.transpose(natural[:, j * P : (j + 1) * P], gain_rows[:, j * P : (j + 1) * P], ident[:])
+            nc.tensor.transpose(by_word[:, j * P : (j + 1) * P], gain_rows[:, j:K_PASS:PACK], ident[:])
+        natural = natural[:].rearrange("p (j b) -> p b j", j=PACK)
+        by_word = by_word[:].rearrange("p (j b) -> p b j", j=PACK)
         size = kept([P, TILES], F32, "size")
         inv_root = kept([P, TILES], F32, "inv_root")
         inv = kept([P, TILES], F32, "inv")
         sign = kept([P, PASSES2, PACK], BF16, "sign")
-        nc.scalar.activation(size[:, 0:PACK], gain_ps[:, 0:PACK], ACT.Abs)
-        nc.scalar.activation(size[:, PACK:TILES], gain_dealt[:, 1, :], ACT.Abs)
+        nc.scalar.activation(size[:, 0:PACK], natural[:, 0, :], ACT.Abs)
+        nc.scalar.activation(size[:, PACK:TILES], by_word[:, 1, :], ACT.Abs)
         nc.scalar.activation(inv_root[:], size[:], ACT.Abs_reciprocal_sqrt, bias=TINY)
         nc.scalar.activation(inv[:], inv_root[:], ACT.Square)
-        nc.scalar.activation(sign[:], gain_dealt[:], ACT.Sign)
+        nc.scalar.activation(sign[:], by_word[:, 0:PASSES2, :], ACT.Sign)
 
         v_words = {}
 
-        def gather_words(a):
-            words = kept([P, S], U32, "v_words_%d" % a)
-            window = tab[a][:].bitcast(U32)
-            if a < PASSES1 - 1:
-                nc.vector.tensor_copy(words[:], window.indirect(offs_sb[:]))
-            for hh in range(HALVES):
-                v_words[a] = words
-            if a == PASSES1 - 1:
-                for first, end in LAST_GATHERS:
-                    part = offs_sb[:, first // LIST_ROWS : end // LIST_ROWS]
-                    nc.vector.tensor_copy(words[:, first:end], window.indirect(part))
+        def gather_words(a, first, end, on=None, pieces=1):
+            v_words[a, first] = kept([P, end - first], U32, "v_words_%d_%d" % (a, first), on)
+            width = (end - first) // pieces
+            for start in range(first, end, width):
+                part = offs_sb[:, start // LIST_ROWS : (start + width) // LIST_ROWS]
+                words = v_words[a, first][:, start - first : start - first + width]
+                nc.vector.tensor_copy(words, tab[a][:].bitcast(U32).indirect(part))
+
+        def gathered(a, first, end):
+            start = first // BANK * BANK if a == PASSES1 - 1 else 0
+            return v_words[a, start][:, first - start : end - start]
 
         planes = kept([P, S], U8, "v_planes")
         nc.vector.tensor_copy(planes[:], tab_plane[:].indirect(offs_sb[:]))
@@ -218,7 +221,7 @@ def tile_list_dye_inhibition_kernel(
                         out=acc[i, hh][:, first - hh * BANK : end - hh * BANK],
                         lhsT=weights[a, i][0].bitcast(FP8X4),
                         lhsT_scale=weights[a, i][1],
-                        rhs=v_words[a][:, first:end].bitcast(FP8X4),
+                        rhs=gathered(a, first, end).bitcast(FP8X4),
                         rhs_scale=planes[4 * a :, first:end],
                         start=(a == 0),
                         stop=(a == PASSES1 - 1 and end % BANK == 0),
@@ -325,13 +328,16 @@ def tile_list_dye_inhibition_kernel(
             )
             return words, plane
 
-        for a in range(PASSES1):
-            gather_words(a)
+        gather_words(0, 0, S)
+        gather_words(1, 0, S)
+        gather_words(2, 0, BANK)
         for i in range(2):
             for a in range(PASSES1):
                 first = kept([P, P, PACK], BF16, "grouped_%d_%d" % (a, i))
                 round_rows(nc.scalar, first[:], a, i)
                 quantise_w1(first[:], "%d_%d" % (a, i), [(a, i)])
+                if (a, i) == (PASSES1 - 1, 0):
+                    gather_words(a, BANK, S, "raw_2_0", 2)
                 stage1(a, [i])
         scores(0, "raw_1_1")
         for a in range(PASSES1):

@@ -76,14 +76,15 @@ def tile_list_dye_inhibition_kernel(
         pos2_sb = lists.tile([P, PAIRS // LIST_ROWS], U16, name="pos2_sb")
         tab_plane = kept([P, T], U8, "tab_plane")
         w2_plane = kept([P, PASSES2, H], U8, "w2_plane")
-        gain_rows = kept([P, K_PASS], F32, "gain_rows")
+        gain_rows = kept([P, P], F32, "gain_rows")
+        gain_dealt = kept([P, PASSES2, PACK], F32, "gain_dealt")
         ident = kept([P, P], F32, "ident")
         warm = kept([P, 2], F32, "warm")
 
+        nc.gpsimd.memset(gain_rows[:], 0.0)
         nc.gpsimd.memset(tab_plane[:].bitcast(I32), 0)
         nc.vector.memset(warm[:], 1.0)
         nc.vector.memset(w2_plane[:].rearrange("p a c -> p (a c)").bitcast(I32), 0)
-        nc.gpsimd.memset(gain_rows[:], 0.0)
         make_identity(nc, ident[:])
 
         nc.scalar.activation(warm[:, 1:2], warm[:, 0:1], ACT.Abs_reciprocal_sqrt)
@@ -107,8 +108,8 @@ def tile_list_dye_inhibition_kernel(
 
         load_table(0)
         nc.sync.dma_start(offs_sb[:], offs)
+        nc.sync.dma_start(out=gain_rows[0:PACK, :], in_=gain[0:K_PASS].rearrange("(i q) -> i q", q=P))
         load_table(1)
-        nc.sync.dma_start(out=gain_rows[0:PASSES2, :], in_=gain.rearrange("(b r) -> b r", r=K_PASS))
         for q in range(P // QUADRANT):
             nc.sync.dma_start(
                 out=tab_plane[:].bitcast(I32)[QUADRANT * q : QUADRANT * q + 4 * PASSES1, :],
@@ -118,6 +119,7 @@ def tile_list_dye_inhibition_kernel(
         load_group(1, 0)
         load_table(2)
         load_group(2, 0)
+        nc.sync.dma_start(out=gain_dealt[:], in_=gain.rearrange("(b p j) -> p b j", p=P, j=PACK))
         nc.sync.dma_start(pos1_sb[:], pos1)
         for g in range(1, PACK):
             for a in range(PASSES1):
@@ -143,22 +145,19 @@ def tile_list_dye_inhibition_kernel(
 
         load_w2(1)
 
-        natural = bank(BANKS - 2, "gain_natural")
-        by_word = bank(BANKS - 1, "gain_by_word")
-        for j in range(PACK):
-            nc.tensor.transpose(natural[:, j * P : (j + 1) * P], gain_rows[:, j * P : (j + 1) * P], ident[:])
-            nc.tensor.transpose(by_word[:, j * P : (j + 1) * P], gain_rows[:, j:K_PASS:PACK], ident[:])
-        natural = natural[:].rearrange("p (j b) -> p b j", j=PACK)
-        by_word = by_word[:].rearrange("p (j b) -> p b j", j=PACK)
-        size = kept([P, TILES], F32, "size")
-        inv_root = kept([P, TILES], F32, "inv_root")
-        inv = kept([P, TILES], F32, "inv")
-        sign = kept([P, PASSES2, PACK], BF16, "sign")
-        nc.scalar.activation(size[:, 0:PACK], natural[:, 0, :], ACT.Abs)
-        nc.scalar.activation(size[:, PACK:TILES], by_word[:, 1, :], ACT.Abs)
-        nc.scalar.activation(inv_root[:], size[:], ACT.Abs_reciprocal_sqrt, bias=TINY)
-        nc.scalar.activation(inv[:], inv_root[:], ACT.Square)
-        nc.scalar.activation(sign[:], by_word[:, 0:PASSES2, :], ACT.Sign)
+        inv = {}
+
+        def invert(gains, name, on=None):
+            size = kept([P, PACK], F32, "size_" + name, on)
+            inv_root = kept([P, PACK], F32, "inv_root_" + name)
+            inv[name] = kept([P, PACK], F32, "inv_" + name)
+            nc.scalar.activation(size[:], gains, ACT.Abs)
+            nc.scalar.activation(inv_root[:], size[:], ACT.Abs_reciprocal_sqrt, bias=TINY)
+            nc.scalar.activation(inv[name][:], inv_root[:], ACT.Square)
+
+        gain_ps = bank(BANKS - 1, "gain_ps")
+        nc.tensor.transpose(gain_ps[:, 0:P], gain_rows[:], ident[:])
+        invert(gain_ps[:, 0:PACK], "natural")
 
         v_words = {}
 
@@ -268,7 +267,7 @@ def tile_list_dye_inhibition_kernel(
             nc.sync.dma_start(out=moved[s][QUADRANT * i : QUADRANT * (i + 1), :, :], in_=root[i][:, halves[s]])
 
         def damping(i, on=None, skip=0):
-            gains = inv[:, i : i + 1]
+            gains = inv["natural" if i < PACK else "dealt"][:, i % PACK : i % PACK + 1]
             if i < PACK:
                 root[i] = kept([P, PAIRS], F32, "root_%d" % i, on, skip)[:]
             else:
@@ -339,6 +338,9 @@ def tile_list_dye_inhibition_kernel(
                 if (a, i) == (PASSES1 - 1, 0):
                     gather_words(a, BANK, S, "raw_2_0", 2)
                 stage1(a, [i])
+        invert(gain_dealt[:, 1, :], "dealt", "raw_0_1")
+        sign = kept([P, PASSES2, PACK], BF16, "sign", "raw_0_1", KIB)
+        nc.scalar.activation(sign[:], gain_dealt[:], ACT.Sign)
         scores(0, "raw_1_1")
         for a in range(PASSES1):
             round_piece(nc.vector, a, 2)

@@ -37,7 +37,7 @@ LAST_GATHERS = ((0, 512), (512, 768), (768, 1024))
 BYTES_OF = {F32: 4, I32: 4, U32: 4, BF16: 2, U16: 2, U8: 1}
 Y_ORDER = (7, 2, 0, 1, 3, 4, 5, 6)
 OUT_ORDER = (7, 0, 1, 2, 3, 4, 5, 6)
-AHEAD = 3
+AHEAD = 6
 Z_PIECES = (((0, 256), (256, 512)), ((0, 256), (256, 384), (384, 512)))
 SPLIT = 1
 
@@ -279,7 +279,7 @@ def tile_list_dye_inhibition_kernel(
 
         sizes = {}
         z_words = {}
-        z_codes = {b: kept([P, PAIRS], U32, "z_codes_%d" % b) for b in range(PASSES2)}
+        z_codes = {1: kept([P, PAIRS], U32, "z_codes_1")}
         z_plane = {b: kept([P, PAIRS], U8, "z_plane_%d" % b) for b in range(PASSES2)}
 
         def interleave(b, s, on=None):
@@ -389,13 +389,14 @@ def tile_list_dye_inhibition_kernel(
             rivals(i, {4: "w2_sb_1", 6: "pair"}.get(i), KIB if i == 6 else 0)
             square(i)
         pick_targets(7, None)
-        pick_targets(0, "pair")
         interleave(0, 0)
         interleave(0, 1)
         signs(0, 0, "pair", 2 * KIB)
         signs(0, 1)
+        z_codes[0] = kept([P, PAIRS], U32, "z_codes_0", "sizes_0_1")
         quantise_z(0, 0)
         quantise_z(0, 1)
+        pick_targets(0, "z_words_0_0")
         dealt_roots = kept([P, PACK, PAIRS], F32, "dealt_roots", "roots")
         for i in dealt:
             damping(i)

@@ -35,11 +35,11 @@ TINY = 1e-30
 KIB = 1024
 LAST_GATHERS = ((0, 512), (512, 768), (768, 1024))
 BYTES_OF = {F32: 4, I32: 4, U32: 4, BF16: 2, U16: 2, U8: 1}
-Y_ORDER = (7, 2, 0, 1, 3, 4, 5, 6)
-OUT_ORDER = (7, 0, 1, 2, 3, 4, 5, 6)
-AHEAD = 6
+Y_ORDER = (0, 2, 1, 3, 4, 5, 6)
+OUT_ORDER = (0, 1, 2, 3, 4, 5, 6)
+SHARED = 7
+AHEAD = 5
 Z_PIECES = (((0, 256), (256, 512)), ((0, 256), (256, 384), (384, 512)))
-SPLIT = 1
 
 
 def tile_list_dye_inhibition_kernel(
@@ -223,7 +223,7 @@ def tile_list_dye_inhibition_kernel(
                         rhs=gathered(a, first, end).bitcast(FP8X4),
                         rhs_scale=planes[4 * a :, first:end],
                         start=(a == 0),
-                        stop=(a == PASSES1 - 1 and end % BANK == 0),
+                        stop=(a == (1 if i == TILES - 1 else PASSES1 - 1) and end % BANK == 0),
                     )
 
         rows = {}
@@ -234,7 +234,8 @@ def tile_list_dye_inhibition_kernel(
             round_rows(engine, rows[i][:, a * P : (a + 1) * P, :], a, i)
 
         def multiply(i):
-            quantise_w1(rows[i][:], str(i), [(a, i) for a in range(PASSES1)])
+            quantise_w1(rows[i][:, 0 : 2 * P, :], "%d_first" % i, [(0, i), (1, i)])
+            quantise_w1(rows[i][:, 2 * P :, :], "%d_last" % i, [(2, i)])
             for a in range(PASSES1):
                 stage1(a, [i])
 
@@ -294,7 +295,7 @@ def tile_list_dye_inhibition_kernel(
         def signs(b, s, on=None, skip=0):
             first, end = Z_PIECES[b][s]
             z_words[b, s] = kept([P, end - first, PACK], BF16, "z_words_%d_%d" % (b, s), on, skip)
-            if (b, s) == (1, 1):
+            if b == 1 and s > 0:
                 room(KIB)
             both = sign[:, b, :].unsqueeze(1).to_broadcast([P, end - first, PACK])
             nc.vector.tensor_tensor(z_words[b, s][:], sizes[b, s][:], both, MULT)
@@ -342,8 +343,9 @@ def tile_list_dye_inhibition_kernel(
         sign = kept([P, PASSES2, PACK], BF16, "sign", "raw_0_1", KIB)
         nc.scalar.activation(sign[:], gain_dealt[:], ACT.Sign)
         scores(0, "raw_1_1")
-        for a in range(PASSES1):
-            round_piece(nc.vector, a, 2)
+        round_piece(nc.vector, 1, 2)
+        round_piece(nc.vector, 2, 2)
+        round_piece(nc.scalar, 0, 2)
         multiply(2)
         rivals(0, "raw_2_2")
         round_piece(nc.scalar, 0, 3)
@@ -366,7 +368,7 @@ def tile_list_dye_inhibition_kernel(
         damping(0, "grouped_0_d", 2 * KIB)
         scores(3, "ahead_d")
         quantise_w1(grouped[1][:], "1_d", [(1, i) for i in dealt])
-        stage1(1, dealt)
+        stage1(1, dealt[:-1])
         rivals(3, "raw_1_d1", 2 * KIB)
         square(2)
         round_dealt(2, 0)
@@ -382,6 +384,7 @@ def tile_list_dye_inhibition_kernel(
         quantise_w1(grouped[2][:, 0 : 2 * P, :], "2_d0", [(2, 4), (2, 5)])
         quantise_w1(grouped[2][:, 2 * P :, :], "2_d1", [(2, 6), (2, 7)])
         stage1(2, dealt)
+        stage1(1, dealt[-1:])
         dealt_words, dealt_plane = deal_w2()
         places["pair"] = room(4 * KIB)
         for i in dealt:
@@ -403,10 +406,11 @@ def tile_list_dye_inhibition_kernel(
 
         y = {}
 
-        def stage2(i, b, cols=slice(0, PAIRS)):
-            start = i not in y
+        def stage2(i, b, cols=slice(0, PAIRS), half=None):
+            key = i if half is None else (i, half)
+            start = key not in y
             if start:
-                y[i] = bank(i, "y_%d" % i)
+                y[key] = bank(i if half is None else i - 1 + half, "y_%d_%d" % (i, cols.start))
             if i < PACK:
                 words = w2_sb[0][:, b, :].bitcast(U8)[:, 2 * i * P : 2 * (i + 1) * P]
                 plane = w2_plane[:, b, i * P : (i + 1) * P]
@@ -415,15 +419,17 @@ def tile_list_dye_inhibition_kernel(
                 words = dealt_words[:, b, t * P : (t + 1) * P].bitcast(U8)
                 plane = dealt_plane[:, b, t * P : (t + 1) * P]
             nc.tensor.matmul_mx(
-                out=y[i][:, cols],
+                out=y[key][:, cols],
                 lhsT=words.bitcast(FP4X4),
                 lhsT_scale=plane,
                 rhs=z_codes[b][:, cols].bitcast(FP8X4),
                 rhs_scale=z_plane[b][:, cols],
                 start=start,
-                stop=(not start and cols.stop == PAIRS),
+                stop=(not start and cols.stop == (HALF if half == 0 else PAIRS)),
             )
 
+        for s in range(2):
+            stage2(SHARED, 0, halves[s], s)
         for i in Y_ORDER[:AHEAD]:
             stage2(i, 0)
         last = range(len(Z_PIECES[1]))
@@ -434,10 +440,9 @@ def tile_list_dye_inhibition_kernel(
             if s + 1 in last:
                 signs(1, s + 1)
             quantise_z(1, s)
-            for i in Y_ORDER[:SPLIT]:
-                stage2(i, 1, slice(*Z_PIECES[1][s]))
+            stage2(SHARED, 1, slice(*Z_PIECES[1][s]), min(s, 1))
         pick_targets(1, "z_words_1_1")
-        for i in Y_ORDER[SPLIT:AHEAD]:
+        for i in Y_ORDER[:AHEAD]:
             stage2(i, 1)
         for i in Y_ORDER[AHEAD:]:
             stage2(i, 1)
@@ -446,6 +451,12 @@ def tile_list_dye_inhibition_kernel(
         results = [kept([P, PACK, PAIRS], F32, "res_%d" % b, None if b == 0 else "tab_2") for b in range(PASSES2)]
         copies = [kept([P, PACK, PAIRS], F32, "y_sb_%d" % b, "tab_%d" % b) for b in range(PASSES2)]
         dealt_out = out[K_PASS:H, :].rearrange("(p t) m -> p t m", t=PACK)
+        shared = kept([P, PAIRS], F32, "res_shared", "z_words_1_2")
+        for s in range(2):
+            y_sb = kept([P, HALF], F32, "y_shared_%d" % s)
+            nc.scalar.copy(y_sb[:], y[SHARED, s][:, halves[s]])
+            nc.gpsimd.tensor_tensor(shared[:, halves[s]], y_sb[:], h2[SHARED][:, halves[s]], MULT)
+        nc.sync.dma_start(out=dealt_out[:, SHARED - PACK, :], in_=shared[:])
         for i in OUT_ORDER:
             b, u = divmod(i, PACK)
             res = results[b][:, u, :]

@@ -205,25 +205,25 @@ def tile_list_dye_inhibition_kernel(
             for u, key in enumerate(keys):
                 weights[key] = (codes[:, u * P : (u + 1) * P], plane[:, u * P : (u + 1) * P])
 
-        def spans(i, a):
-            if (i, a) == (0, PASSES1 - 1):
+        def spans(i):
+            if i == 0:
                 return LAST_GATHERS
             return [(hh * BANK, (hh + 1) * BANK) for hh in range(HALVES)]
 
         def stage1(a, tiles):
             for i in tiles:
-                for first, end in spans(i, a):
-                    hh = first // BANK
+                for n, (first, end) in enumerate(spans(i)):
                     if a == 0:
-                        acc[i, hh] = bank((HALVES * i + hh) % BANKS, "acc_%d_%d" % (i, hh))
+                        index = HALVES * i + n if n < HALVES else BANKS - 1
+                        acc[i, n] = bank(index % BANKS, "acc_%d_%d" % (i, n))
                     nc.tensor.matmul_mx(
-                        out=acc[i, hh][:, first - hh * BANK : end - hh * BANK],
+                        out=acc[i, n][:, 0 : end - first],
                         lhsT=weights[a, i][0].bitcast(FP8X4),
                         lhsT_scale=weights[a, i][1],
                         rhs=gathered(a, first, end).bitcast(FP8X4),
                         rhs_scale=planes[4 * a :, first:end],
                         start=(a == 0),
-                        stop=(a == (1 if i == TILES - 1 else PASSES1 - 1) and end % BANK == 0),
+                        stop=(a == (1 if i == TILES - 1 else PASSES1 - 1)),
                     )
 
         rows = {}
@@ -247,8 +247,8 @@ def tile_list_dye_inhibition_kernel(
 
         def scores(i, on=None):
             h[i] = kept([P, S], F32, "h_%d" % i, on)
-            for hh in range(HALVES):
-                nc.scalar.copy(h[i][:, hh * BANK : (hh + 1) * BANK], acc[i, hh][:])
+            for n, (first, end) in enumerate(spans(i)):
+                nc.scalar.copy(h[i][:, first:end], acc[i, n][:, 0 : end - first])
 
         def rivals(i, on=None, skip=0):
             x[i] = kept([P, PAIRS], F32, "x_%d" % i, on, skip)
@@ -343,9 +343,8 @@ def tile_list_dye_inhibition_kernel(
         sign = kept([P, PASSES2, PACK], BF16, "sign", "raw_0_1", KIB)
         nc.scalar.activation(sign[:], gain_dealt[:], ACT.Sign)
         scores(0, "raw_1_1")
-        round_piece(nc.vector, 1, 2)
-        round_piece(nc.vector, 2, 2)
-        round_piece(nc.scalar, 0, 2)
+        for a in range(PASSES1):
+            round_piece(nc.vector, a, 2)
         multiply(2)
         rivals(0, "raw_2_2")
         round_piece(nc.scalar, 0, 3)

from contextlib import ExitStack

import concourse.mybir as mybir
from concourse.masks import make_identity

T, S, PAIRS, K, H = 2048, 1024, 512, 1536, 1024
FLOPS = 2 * K * H * S + 2 * H * H * PAIRS

F32 = mybir.dt.float32
BF16 = mybir.dt.bfloat16
I32 = mybir.dt.int32
U32 = mybir.dt.uint32
U16 = mybir.dt.uint16
U8 = mybir.dt.uint8
FP8X4 = mybir.dt.float8_e4m3fn_x4
FP4X4 = mybir.dt.float4_e2m1fn_x4
ACT = mybir.ActivationFunctionType
MULT = mybir.AluOpType.mult

P = 128
PACK = 4
K_PASS = P * PACK
BANK = 512
BANKS = 8
QUADRANT = 32
LIST_ROWS = 16
LINE = 16
PASSES1 = K // K_PASS
PASSES2 = H // K_PASS
TILES = H // P
HALVES = S // BANK
HALF = PAIRS // 2
WALK = 4
TINY = 1e-30
KIB = 1024
LAST_GATHERS = ((0, 512), (512, 768), (768, 1024))
BYTES_OF = {F32: 4, I32: 4, U32: 4, BF16: 2, U16: 2, U8: 1}
Y_ORDER = (0, 2, 1, 3, 4, 5, 6)
OUT_ORDER = (0, 1, 2, 3, 4, 5, 6)
SHARED = 7
AHEAD = 5
Z_PIECES = (((0, 256), (256, 512)), ((0, 256), (256, 384), (384, 512)))


def tile_list_dye_inhibition_kernel(
    tc, tab_words, tab_scales, offs, pos1, pos2, w1, gain, w2_words, w2_scales, out
):
    nc = tc.nc
    with ExitStack() as ctx:
        lists = ctx.enter_context(tc.tile_pool(name="lists", bufs=1))
        keep = ctx.enter_context(tc.tile_pool(name="keep", bufs=1))
        psum = ctx.enter_context(tc.psum_pool(name="psum", bufs=1))

        places = {"end": 0}

        def room(size):
            first = places["end"]
            places["end"] = first + (size + 63) // 64 * 64
            return first

        def kept(shape, dtype, name, on=None, skip=0):
            if on is None:
                size = BYTES_OF[dtype]
                for n in shape[1:]:
                    size = size * n
                places[name] = room(size)
            else:
                places[name] = places[on] + skip
            return keep.tile(shape, dtype, name=name, tag=name, align_bytes=64, offset=places[name])

        def bank(index, name):
            return psum.tile([P, BANK], F32, name=name, tag="bank%d" % index)

        offs_sb = lists.tile([P, S // LIST_ROWS], U16, name="offs_sb")
        pos1_sb = lists.tile([P, PAIRS // LIST_ROWS], U16, name="pos1_sb")
        pos2_sb = lists.tile([P, PAIRS // LIST_ROWS], U16, name="pos2_sb")
        tab_plane = kept([P, T], U8, "tab_plane")
        w2_plane = kept([P, PASSES2, H], U8, "w2_plane")
        gain_rows = kept([P, P], F32, "gain_rows")
        gain_dealt = kept([P, PASSES2, PACK], F32, "gain_dealt")
        ident = kept([P, P], F32, "ident")
        warm = kept([P, 2], F32, "warm")

        nc.gpsimd.memset(gain_rows[:], 0.0)
        nc.gpsimd.memset(tab_plane[:].bitcast(I32), 0)
        nc.vector.memset(warm[:], 1.0)
        nc.vector.memset(w2_plane[:].rearrange("p a c -> p (a c)").bitcast(I32), 0)
        make_identity(nc, ident[:])

        nc.scalar.activation(warm[:, 1:2], warm[:, 0:1], ACT.Abs_reciprocal_sqrt)

        tab = {}
        raw = {}

        def load_w1(a, key, first, end, on=None, skip=0):
            raw[a, key] = kept([P, PACK, end - first], F32, "raw_%d_%s" % (a, key), on, skip)
            rows = w1[a * K_PASS : (a + 1) * K_PASS, first:end]
            nc.sync.dma_start(out=raw[a, key][:], in_=rows.rearrange("(p j) c -> p j c", j=PACK))

        def load_group(a, g):
            if g == PACK - 1 and a != 1:
                places["ahead_%d" % a] = room((2 - a // 2) * KIB)
            load_w1(a, str(g), g * P, (g + 1) * P)

        def load_table(a):
            tab[a] = kept([P, T], I32, "tab_%d" % a)
            nc.sync.dma_start(out=tab[a][:], in_=tab_words[a].rearrange("p t i -> p (t i)").bitcast(I32))

        load_table(0)
        nc.sync.dma_start(offs_sb[:], offs)
        nc.sync.dma_start(out=gain_rows[0:PACK, :], in_=gain[0:K_PASS].rearrange("(i q) -> i q", q=P))
        load_table(1)
        for q in range(P // QUADRANT):
            nc.sync.dma_start(
                out=tab_plane[:].bitcast(I32)[QUADRANT * q : QUADRANT * q + 4 * PASSES1, :],
                in_=tab_scales.bitcast(I32)[:, 4 * q : 4 * q + 4, :],
            )
        load_group(0, 0)
        load_group(1, 0)
        load_table(2)
        load_group(2, 0)
        nc.sync.dma_start(out=gain_dealt[:], in_=gain.rearrange("(b p j) -> p b j", p=P, j=PACK))
        nc.sync.dma_start(pos1_sb[:], pos1)
        for g in range(1, PACK):
            for a in range(PASSES1):
                load_group(a, g)
        room(KIB)
        nc.sync.dma_start(pos2_sb[:], pos2)
        for a in range(PASSES1):
            for s in range(2):
                if (a, s) == (1, 0):
                    places["ahead_d"] = room(2 * KIB)
                load_w1(a, "d%d" % s, K_PASS + s * K_PASS // 2, K_PASS + (s + 1) * K_PASS // 2)
        for q in range(P // QUADRANT):
            nc.sync.dma_start(
                out=w2_plane[:].bitcast(I32)[QUADRANT * q : QUADRANT * q + 4, :, :],
                in_=w2_scales.bitcast(I32)[:, 4 * q : 4 * q + 4, :].rearrange("a r c -> r a c"),
            )
        w2_sb = {}

        def load_w2(s, on=None):
            w2_sb[s] = kept([P, PASSES2, H // 4], I32, "w2_sb_%d" % s, on)
            cols = w2_words.bitcast(I32)[:, :, s * H // 4 : (s + 1) * H // 4]
            nc.sync.dma_start(out=w2_sb[s][:], in_=cols.rearrange("a p c -> p a c"))

        load_w2(1)

        inv = {}

        def invert(gains, name, on=None):
            size = kept([P, PACK], F32, "size_" + name, on)
            inv_root = kept([P, PACK], F32, "inv_root_" + name)
            inv[name] = kept([P, PACK], F32, "inv_" + name)
            nc.scalar.activation(size[:], gains, ACT.Abs)
            nc.scalar.activation(inv_root[:], size[:], ACT.Abs_reciprocal_sqrt, bias=TINY)
            nc.scalar.activation(inv[name][:], inv_root[:], ACT.Square)

        gain_ps = bank(BANKS - 1, "gain_ps")
        nc.tensor.transpose(gain_ps[:, 0:P], gain_rows[:], ident[:])
        invert(gain_ps[:, 0:PACK], "natural")

        v_words = {}

        def gather_words(a, first, end, on=None, pieces=1):
            v_words[a, first] = kept([P, end - first], U32, "v_words_%d_%d" % (a, first), on)
            width = (end - first) // pieces
            for start in range(first, end, width):
                part = offs_sb[:, start // LIST_ROWS : (start + width) // LIST_ROWS]
                words = v_words[a, first][:, start - first : start - first + width]
                nc.vector.tensor_copy(words, tab[a][:].bitcast(U32).indirect(part))

        def gathered(a, first, end):
            start = first // BANK * BANK if a == PASSES1 - 1 else 0
            return v_words[a, start][:, first - start : end - start]

        planes = kept([P, S], U8, "v_planes")
        nc.vector.tensor_copy(planes[:], tab_plane[:].indirect(offs_sb[:]))

        grouped = {}
        weights = {}
        acc = {}

        def round_rows(engine, dst, a, g):
            dst = dst.rearrange("p (c i) j -> p c j i", i=WALK)
            src = raw[a, str(g)][:].rearrange("p j (c i) -> p c j i", i=WALK)
            if engine is nc.vector:
                nc.vector.tensor_copy(dst, src)
            else:
                nc.scalar.copy(dst, src)

        def round_dealt(a, s):
            if s == 0:
                grouped[a] = kept([P, K_PASS, PACK], BF16, "grouped_%d_d" % a)
            dst = grouped[a][:].rearrange("p (t m) j -> p m j t", m=P)[:, s * P // 2 : (s + 1) * P // 2, :, :]
            src = raw[a, "d%d" % s][:].rearrange("p j (m t) -> p m j t", t=PACK)
            if s == 1:
                nc.vector.tensor_copy(dst, src)
            else:
                nc.scalar.copy(dst, src)

        def quantise_w1(rows, name, keys):
            codes = kept([P, len(keys) * P], U32, "w_codes_" + name)
            plane = kept([P, len(keys) * P], U8, "w_plane_" + name)
            nc.vector.quantize_mx(out=codes[:].bitcast(FP8X4), scales=plane[:], in_=rows.rearrange("p c j -> p (c j)"))
            for u, key in enumerate(keys):
                weights[key] = (codes[:, u * P : (u + 1) * P], plane[:, u * P : (u + 1) * P])

        def spans(i):
            if i == 0:
                return LAST_GATHERS
            return [(hh * BANK, (hh + 1) * BANK) for hh in range(HALVES)]

        def stage1(a, tiles):
            for i in tiles:
                for n, (first, end) in enumerate(spans(i)):
                    if a == 0:
                        index = HALVES * i + n if n < HALVES else BANKS - 1
                        acc[i, n] = bank(index % BANKS, "acc_%d_%d" % (i, n))
                    nc.tensor.matmul_mx(
                        out=acc[i, n][:, 0 : end - first],
                        lhsT=weights[a, i][0].bitcast(FP8X4),
                        lhsT_scale=weights[a, i][1],
                        rhs=gathered(a, first, end).bitcast(FP8X4),
                        rhs_scale=planes[4 * a :, first:end],
                        start=(a == 0),
                        stop=(a == (1 if i == TILES - 1 else PASSES1 - 1)),
                    )

        rows = {}

        def round_piece(engine, a, i):
            if i not in rows:
                rows[i] = kept([P, PASSES1 * P, PACK], BF16, "grouped_%d" % i)
            round_rows(engine, rows[i][:, a * P : (a + 1) * P, :], a, i)

        def multiply(i):
            quantise_w1(rows[i][:, 0 : 2 * P, :], "%d_first" % i, [(0, i), (1, i)])
            quantise_w1(rows[i][:, 2 * P :, :], "%d_last" % i, [(2, i)])
            for a in range(PASSES1):
                stage1(a, [i])

        h = {}
        x = {}
        sq = {}
        places["roots"] = room(8 * KIB)
        moved = {0: kept([P, PACK, HALF], F32, "moved_0", "roots")}

        def scores(i, on=None):
            h[i] = kept([P, S], F32, "h_%d" % i, on)
            for n, (first, end) in enumerate(spans(i)):
                nc.scalar.copy(h[i][:, first:end], acc[i, n][:, 0 : end - first])

        def rivals(i, on=None, skip=0):
            x[i] = kept([P, PAIRS], F32, "x_%d" % i, on, skip)
            nc.vector.tensor_copy(x[i][:], h[i][:].indirect(pos1_sb[:]))

        def square(i, on=None, skip=0):
            sq[i] = kept([P, PAIRS], F32, "sq_%d" % i, on, skip)
            if i == PACK - 1:
                nc.scalar.activation(sq[i][:], x[i][:], ACT.Square)
            else:
                nc.gpsimd.tensor_tensor(sq[i][:], x[i][:], x[i][:], MULT)

        root = {}
        halves = (slice(0, HALF), slice(HALF, PAIRS))

        def move(i, s):
            nc.sync.dma_start(out=moved[s][QUADRANT * i : QUADRANT * (i + 1), :, :], in_=root[i][:, halves[s]])

        def damping(i, on=None, skip=0):
            gains = inv["natural" if i < PACK else "dealt"][:, i % PACK : i % PACK + 1]
            if i < PACK:
                root[i] = kept([P, PAIRS], F32, "root_%d" % i, on, skip)[:]
            else:
                root[i] = dealt_roots[:, i - PACK, :]
            for cols in halves if i % PACK == PACK - 1 else [slice(0, PAIRS)]:
                nc.scalar.activation(root[i][:, cols], sq[i][:, cols], ACT.Abs_reciprocal_sqrt, bias=gains, scale=gains)
            if i < PACK:
                move(i, 0)

        sizes = {}
        z_words = {}
        z_codes = {1: kept([P, PAIRS], U32, "z_codes_1")}
        z_plane = {b: kept([P, PAIRS], U8, "z_plane_%d" % b) for b in range(PASSES2)}

        def interleave(b, s, on=None):
            first, end = Z_PIECES[b][s]
            sizes[b, s] = kept([P, end - first, PACK], BF16, "sizes_%d_%d" % (b, s), on)
            nc.scalar.activation(
                sizes[b, s][:].rearrange("p (c i) j -> p c j i", i=WALK),
                (moved[s][:] if b == 0 else dealt_roots[:, :, first:end]).rearrange("p j (c i) -> p c j i", i=WALK),
                ACT.Square,
            )

        def signs(b, s, on=None, skip=0):
            first, end = Z_PIECES[b][s]
            z_words[b, s] = kept([P, end - first, PACK], BF16, "z_words_%d_%d" % (b, s), on, skip)
            if b == 1 and s > 0:
                room(KIB)
            both = sign[:, b, :].unsqueeze(1).to_broadcast([P, end - first, PACK])
            nc.vector.tensor_tensor(z_words[b, s][:], sizes[b, s][:], both, MULT)

        def quantise_z(b, s):
            cols = slice(*Z_PIECES[b][s])
            nc.vector.quantize_mx(
                out=z_codes[b][:, cols].bitcast(FP8X4),
                scales=z_plane[b][:, cols],
                in_=z_words[b, s][:].rearrange("p c j -> p (c j)"),
            )

        h2 = {}

        def pick_targets(i, on, skip=0):
            h2[i] = kept([P, PAIRS], F32, "h2_%d" % i, on, skip)
            nc.vector.tensor_copy(h2[i][:], h[i][:].indirect(pos2_sb[:]))

        def deal_w2():
            words = kept([P, PASSES2, K_PASS], U16, "w2_dealt_words", "grouped_2_d")
            plane = kept([P, PASSES2, K_PASS], U8, "w2_dealt_plane", "grouped_2_d", 2 * KIB)
            n = LINE // 2
            nc.vector.tensor_copy(
                plane[:].rearrange("p b (t c i) -> p b c t i", t=PACK, i=LINE),
                w2_plane[:, :, K_PASS:H].rearrange("p b (c i t) -> p b c t i", t=PACK, i=LINE),
            )
            nc.vector.tensor_copy(
                words[:].rearrange("p b (t c i) -> p b c t i", t=PACK, i=n),
                w2_sb[1][:].bitcast(U16).rearrange("p b (c i t) -> p b c t i", t=PACK, i=n),
            )
            return words, plane

        gather_words(0, 0, S)
        gather_words(1, 0, S)
        gather_words(2, 0, BANK)
        for i in range(2):
            for a in range(PASSES1):
                first = kept([P, P, PACK], BF16, "grouped_%d_%d" % (a, i))
                round_rows(nc.scalar, first[:], a, i)
                quantise_w1(first[:], "%d_%d" % (a, i), [(a, i)])
                if (a, i) == (PASSES1 - 1, 0):
                    gather_words(a, BANK, S, "raw_2_0", 2)
                stage1(a, [i])
        invert(gain_dealt[:, 1, :], "dealt", "raw_0_1")
        sign = kept([P, PASSES2, PACK], BF16, "sign", "raw_0_1", KIB)
        nc.scalar.activation(sign[:], gain_dealt[:], ACT.Sign)
        scores(0, "raw_1_1")
        for a in range(PASSES1):
            round_piece(nc.vector, a, 2)
        multiply(2)
        rivals(0, "raw_2_2")
        round_piece(nc.scalar, 0, 3)
        round_piece(nc.scalar, 1, 3)
        round_piece(nc.vector, 2, 3)
        scores(1, "ahead_0")
        multiply(3)
        rivals(1, "ahead_2")
        square(0, "ahead_2", 2 * KIB)
        dealt = range(PACK, TILES)
        round_dealt(0, 0)
        round_dealt(0, 1)
        scores(2)
        quantise_w1(grouped[0][:], "0_d", [(0, i) for i in dealt])
        stage1(0, dealt)
        round_dealt(1, 0)
        round_dealt(1, 1)
        rivals(2, "raw_1_d0", 2 * KIB)
        square(1, "grouped_0_d")
        damping(0, "grouped_0_d", 2 * KIB)
        scores(3, "ahead_d")
        quantise_w1(grouped[1][:], "1_d", [(1, i) for i in dealt])
        stage1(1, dealt[:-1])
        rivals(3, "raw_1_d1", 2 * KIB)
        square(2)
        round_dealt(2, 0)
        round_dealt(2, 1)
        damping(1)
        square(3, "roots", 4 * KIB)
        damping(2)
        damping(3)
        moved[1] = kept([P, PACK, HALF], F32, "moved_1", "roots", 4 * KIB)
        for i in range(PACK):
            move(i, 1)
        load_w2(0, "root_3")
        quantise_w1(grouped[2][:, 0 : 2 * P, :], "2_d0", [(2, 4), (2, 5)])
        quantise_w1(grouped[2][:, 2 * P :, :], "2_d1", [(2, 6), (2, 7)])
        stage1(2, dealt)
        stage1(1, dealt[-1:])
        dealt_words, dealt_plane = deal_w2()
        places["pair"] = room(4 * KIB)
        for i in dealt:
            scores(i)
            rivals(i, {4: "w2_sb_1", 6: "pair"}.get(i), KIB if i == 6 else 0)
            square(i)
        pick_targets(7, None)
        interleave(0, 0)
        interleave(0, 1)
        signs(0, 0, "pair", 2 * KIB)
        signs(0, 1)
        z_codes[0] = kept([P, PAIRS], U32, "z_codes_0", "sizes_0_1")
        quantise_z(0, 0)
        quantise_z(0, 1)
        pick_targets(0, "z_words_0_0")
        dealt_roots = kept([P, PACK, PAIRS], F32, "dealt_roots", "roots")
        for i in dealt:
            damping(i)

        y = {}

        def stage2(i, b, cols=slice(0, PAIRS), half=None):
            key = i if half is None else (i, half)
            start = key not in y
            if start:
                y[key] = bank(i if half is None else i - 1 + half, "y_%d_%d" % (i, cols.start))
            if i < PACK:
                words = w2_sb[0][:, b, :].bitcast(U8)[:, 2 * i * P : 2 * (i + 1) * P]
                plane = w2_plane[:, b, i * P : (i + 1) * P]
            else:
                t = i - PACK
                words = dealt_words[:, b, t * P : (t + 1) * P].bitcast(U8)
                plane = dealt_plane[:, b, t * P : (t + 1) * P]
            nc.tensor.matmul_mx(
                out=y[key][:, cols],
                lhsT=words.bitcast(FP4X4),
                lhsT_scale=plane,
                rhs=z_codes[b][:, cols].bitcast(FP8X4),
                rhs_scale=z_plane[b][:, cols],
                start=start,
                stop=(not start and cols.stop == (HALF if half == 0 else PAIRS)),
            )

        for s in range(2):
            stage2(SHARED, 0, halves[s], s)
        for i in Y_ORDER[:AHEAD]:
            stage2(i, 0)
        last = range(len(Z_PIECES[1]))
        for s in last:
            interleave(1, s)
        signs(1, 0)
        for s in last:
            if s + 1 in last:
                signs(1, s + 1)
            quantise_z(1, s)
            stage2(SHARED, 1, slice(*Z_PIECES[1][s]), min(s, 1))
        pick_targets(1, "z_words_1_1")
        for i in Y_ORDER[:AHEAD]:
            stage2(i, 1)
        for i in Y_ORDER[AHEAD:]:
            stage2(i, 1)
            stage2(i, 0)

        results = [kept([P, PACK, PAIRS], F32, "res_%d" % b, None if b == 0 else "tab_2") for b in range(PASSES2)]
        copies = [kept([P, PACK, PAIRS], F32, "y_sb_%d" % b, "tab_%d" % b) for b in range(PASSES2)]
        dealt_out = out[K_PASS:H, :].rearrange("(p t) m -> p t m", t=PACK)
        shared = kept([P, PAIRS], F32, "res_shared", "z_words_1_2")
        for s in range(2):
            y_sb = kept([P, HALF], F32, "y_shared_%d" % s)
            nc.scalar.copy(y_sb[:], y[SHARED, s][:, halves[s]])
            nc.gpsimd.tensor_tensor(shared[:, halves[s]], y_sb[:], h2[SHARED][:, halves[s]], MULT)
        nc.sync.dma_start(out=dealt_out[:, SHARED - PACK, :], in_=shared[:])
        for i in OUT_ORDER:
            b, u = divmod(i, PACK)
            res = results[b][:, u, :]
            rows = out[i * P : (i + 1) * P, :] if b == 0 else dealt_out[:, u, :]
            if i in h2:
                nc.vector.tensor_tensor(res, y[i][:], h2[i][:], MULT)
                nc.sync.dma_start(out=rows, in_=res)
            else:
                y_sb = copies[b][:, u, :]
                nc.scalar.copy(y_sb, y[i][:])
                parts = 2 if i == OUT_ORDER[-1] else 1
                for s in range(parts):
                    first, end = s * PAIRS // parts, (s + 1) * PAIRS // parts
                    targets = h[i][:].indirect(pos2_sb[:, first // LIST_ROWS : end // LIST_ROWS])
                    nc.vector.tensor_tensor(res[:, first:end], targets, y_sb[:, first:end], MULT)
                    nc.sync.dma_start(out=rows[:, first:end], in_=res[:, first:end])
